import numpy as np, ml_dtypes
CORES = [40,64,80,88,96,104,120,144]
N = 8
T, EL, CAP, CAPP = 4096, 2, 1920, 512
E = N * EL
def entries(a): return a.T.reshape(-1)
def pack(v, P): return np.ascontiguousarray(np.asarray(v, np.int32).reshape(-1, P).T)
def lists(rng, how):
    g, q, h, R, K = CAP // CAPP, CAP % CAPP, E // 4, np.arange(N)[:, None], np.arange(E)
    C = np.zeros((N, E), np.int64); s = rng.integers(1, E, N); S = None
    few = rng.integers(1, CAPP // 4 + 1, (N, h)); t = rng.integers(CAPP // 8, 3 * CAPP // 8 + 1, (N, 3)); t[:, 2] = CAPP - t[:, 0] - t[:, 1]
    if how == "uniform":
        C[:, :h] = np.where(R <= g, CAPP, few); C[:, h:] = rng.integers(0, CAP // (2 * N) + 1, (N, E - h)); S = np.stack([rng.permutation(2 * h)[:3] + 1 for r in range(N)])
    if how == "bands":
        a = np.arange(E) % N; C = CAPP * ((R >= a) & (R <= a + g)); C[a[N:], np.arange(N, E)] = rng.integers(1, CAPP + 1, E - N); s[g:] = N - g + rng.integers(0, g, N - g) - np.arange(N - g)
    if how == "full":
        v = rng.integers(CAPP - q + 1, CAPP, h + 1); C[:, :h] = CAPP; C[:, h:2 * h + 1] = (CAP - v) // N; C[rng.integers(N), h:2 * h + 1] += (CAP - v) % N; s = h + (np.arange(N) + rng.integers(2)) % 2
    if how == "late":
        C[:N - 1, :h] = np.where(R <= g, CAPP, few)[:N - 1]; C[N - 1, h:3 * h] = rng.integers(1, CAPP + 1, 2 * h); s = rng.integers(h, 2 * h + 1, N)
    if how == "mesh":
        ev = np.arange(0, E, 2); P = np.stack([rng.permutation(2 * h) for r in range(N)]); S = 2 * P[:, :3] + 1; S[g] = 2 * rng.permutation(2 * h - 1)[:3] + 2
        C[:, ev] = CAPP; C[g, ev[h:]] = q; C[g, ev + 1] = rng.integers(0, (CAPP - q) // 2 + 1, 2 * h); C[g, 1] = 0
        z, y = g + 1 + int(rng.integers(0, g - 1)), 2 * int(rng.integers(1, 2 * h)) + 1; C[z, (y - 2 * P[z, 3] - 1) % E] = 0; C[z, y] = CAPP
    if how == "thin":
        C = rng.integers(0, CAP // N + 1, (N, E)); C[1] = 1; C[[0, N // 2, N - 1]] = 0
    if S is None: S, t = s[:, None], np.full((N, 1), CAPP)
    D = np.zeros((N, E, E), np.int64); Z = C.copy()
    for j in range(S.shape[1]):
        w = rng.integers(np.maximum(Z - t[:, j + 1:].sum(axis=1)[:, None], 0), np.minimum(Z, t[:, j:j + 1]) + 1); D[R, K, (K + S[:, j:j + 1]) % E] = w; Z -= w
    X = np.stack([rng.permutation(np.concatenate([np.repeat(np.arange(E * E), D[r].reshape(-1)), np.full(T - D[r].sum(), -1)])) for r in range(N)]); c = np.append(rng.permutation(E), -1)
    return {"e1": np.stack([pack(w, 16) for w in c[X // E]]), "e2": np.stack([pack(w, 16) for w in c[np.where(X < 0, -1, X % E)]])}
def blank(d):
    for r in range(0, N, 2):
        u, i = np.unique(entries(d["e1"][r])[::-1], return_index=True); d["x"][r][:, T - 1 - i[u >= 0]] = 0
def setup_inputs(rng):
    return dict({"x": rng.standard_normal((N, 128, T), dtype=np.float32).astype(ml_dtypes.bfloat16)}, **lists(rng, "uniform"))
def setup_inputs_bands(rng):
    d = setup_inputs(rng); d.update(lists(rng, "bands"))
    for k in ("x",): d[k] = (d[k].astype(np.float32) * 1048576.0).astype(d[k].dtype)
    blank(d)
    return d
def setup_inputs_full(rng):
    d = setup_inputs(rng); d.update(lists(rng, "full"))
    for k in ("x",): d[k] = (d[k].astype(np.float32) * (1 / 1024.0)).astype(d[k].dtype)
    blank(d)
    return d
def setup_inputs_late(rng):
    d = setup_inputs(rng); d.update(lists(rng, "late"))
    blank(d)
    return d
def setup_inputs_mesh(rng):
    d = setup_inputs(rng); d.update(lists(rng, "mesh"))
    blank(d)
    return d
def setup_inputs_thin(rng):
    d = setup_inputs(rng); d.update(lists(rng, "thin"))
    blank(d)
    return d
def check_inputs(x):
    bad = []; a, b = x["e1"], x["e2"]
    if min(a.min(), b.min()) < -1 or max(a.max(), b.max()) >= E: bad.append("e1 or e2 out of range")
    if ((a < 0) != (b < 0)).any(): bad.append("-1 stands in one of e1 and e2 alone")
    if ((a == b) & (a >= 0)).any(): bad.append("a token's two choices are one expert")
    if max(int(np.bincount(v[v >= 0], minlength=E).max()) for w in (a, b) for v in w) > CAPP: bad.append("more than CAPP tokens of one rank have one expert as first choice, or as second choice")
    return bad
def places(e):
    o = np.argsort(e, kind="stable"); p = np.empty(len(e), np.int64); p[o] = np.arange(len(e)) - np.searchsorted(e[o], e[o]); return p
def reference(x, e1, e2):
    X = np.concatenate(list(x), axis=1); a, b = [np.concatenate([entries(v) for v in w]) for w in (e1, e2)]
    k = np.nonzero(a >= 0)[0]; p = places(a[k])
    c1 = np.minimum(np.bincount(a[k], minlength=E), CAP)
    f = k[p >= CAP]; u = c1[b[f]] + places(b[f])
    Y = np.zeros((128, E * CAP), x.dtype); m = p < CAP; Y[:, CAP * a[k[m]] + p[m]] = X[:, k[m]]
    n = u < CAP; Y[:, CAP * b[f[n]] + u[n]] = X[:, f[n]]
    return {"y": np.stack([Y[:, EL * CAP * r:EL * CAP * (r + 1)] for r in range(N)])}

@@ -1,0 +1,537 @@
+from concourse.bass import DstId, RemoteDMATransfer
+from concourse.mybir import AluOpType as A, AxisListType, ActivationFunctionType as AF
+
+NS, SW = 8, 514
+BLK, HEAD = NS * SW, 16
+HALF = 2048
+WIN = HEAD + 8 * BLK
+NEV = 72
+
+SCRATCH = {
+    "win": ("sbuf", [128, WIN], "bfloat16"),
+    "yo": ("sbuf", [128, 3840], "bfloat16"),
+    "eb": ("sbuf", [128, 64], "int32"),
+    "ifq": ("sbuf", [128, 128], "int32"), "iq": ("sbuf", [128, 1], "int32"), "cib": ("sbuf", [128, 32], "int32"),
+    "ti": ("sbuf", [128, 8], "int32"), "tf": ("sbuf", [128, 48], "float32"), "pmi": ("sbuf", [128, 128], "int32"),
+    "gfi": ("sbuf", [128, 128], "int32"),
+    "d2": ("sbuf", [128, 128], "float16"), "dm": ("sbuf", [128, 128], "float16"),
+    "mats": ("sbuf", [128, 1024], "float16"), "rot": ("sbuf", [128, 2048], "float16"),
+    "sel": ("sbuf", [128, 256], "float32"),
+    "ci": ("sbuf", [128, 32], "float32"), "cj": ("sbuf", [128, 32], "float32"), "ix": ("sbuf", [128, 32], "uint16"),
+    "si": ("sbuf", [128, 12], "int32"), "tm": ("sbuf", [128, 32], "float32"),
+    "cc": ("sbuf", [128, 32], "float32"), "cn": ("sbuf", [128, 16], "float32"), "cs": ("sbuf", [128, 4], "float32"),
+    "ls": ("sbuf", [128, 1024], "float16"), "lw": ("sbuf", [128, 136], "float32"),
+    "gg": ("sbuf", [128, 512], "float16"), "gp": ("sbuf", [128, 512], "float16"),
+    "ofs": ("sbuf", [128, 240], "uint16"),
+    "ef": ("sbuf", [128, 64], "float16"), "er": ("sbuf", [128, 512], "bfloat16"),
+    "bo": ("sbuf", [128, 128], "float16"), "up": ("sbuf", [128, 128], "float16"), "u1": ("sbuf", [128, 128], "float16"),
+    "gs": ("sbuf", [128, 128], "float16"), "gt": ("sbuf", [128, 16], "float16"), "idb": ("sbuf", [128, 128], "bfloat16"),
+    "idf": ("sbuf", [128, 128], "float32"), "iot": ("sbuf", [128, 128], "float16"), "val": ("sbuf", [128, 32], "float32"),
+    "mm": ("sbuf", [128, 512], "float16"), "cu": ("sbuf", [128, 512], "float16"), "v1": ("sbuf", [128, 512], "float16"),
+    "ff": ("sbuf", [128, 512], "float16"), "m2": ("sbuf", [128, 512], "float16"), "c2": ("sbuf", [128, 512], "float16"),
+    "v2": ("sbuf", [128, 512], "float16"),
+    "ki": ("sbuf", [128, 512], "int32"), "kf": ("sbuf", [128, 512], "float32"),
+    "oh": ("sbuf", [128, 4096], "float16"), "ol": ("sbuf", [128, 4096], "float16"), "lf": ("sbuf", [128, 128], "float16"),
+}
+for _n in "abcdefgh":
+    SCRATCH["p" + _n] = ("psum", [128, 512], "float32")
+SEMAPHORES = (["x%d_%d" % (s, h) for s in range(8) for h in range(NS)] + ["e%d" % i for i in range(NEV)]
+              + ["xin", "ein", "cnt1", "cnt2", "lists", "sent"])
+
+_PLAN = {}
+
+
+def _bits(m):
+    return bin(m).count("1")
+
+
+def _plan(T, topo):
+    if _PLAN:
+        return _PLAN
+    R, n = list(T.cores), len(T.cores)
+    everyone = range(256)
+    chip = [[c for c in everyone if topo.host(c) == topo.host(R[r]) and topo.chip(c) == topo.chip(R[r])] for r in range(n)]
+    mate = [[c for c in everyone if topo.mates(c, R[r])] for r in range(n)]
+    pair = [([u for u in range(n) if R[u] in mate[r]] + [None])[0] for r in range(n)]
+    near = [[c for c in chip[r] if topo.die(c) == topo.die(R[r]) and c != R[r]] for r in range(n)]
+    brain = [[c for c in near[r] if topo.may_write(c, mate[r][0])][0] for r in range(n)]
+    owner = []
+    for r in range(n):
+        p = [c for c in near[r] if not topo.may_write(c, mate[r][0])][0]
+        m = [c for c in near[r] if c not in (p, brain[r])][0]
+        far = [c for c in chip[r] if topo.die(c) != topo.die(R[r])]
+        owner.append(([p, p, R[r], R[r]] if pair[r] is not None else [p, p, m, R[r]]) + far)
+    sends, fwd, xin = {}, {}, [0] * n
+    for s in range(n):
+        plane = [t for t in range(n) if t == s or topo.same_plane(R[s], R[t])]
+        turn = plane.index(s)
+        cross = [t for t in range(n) if t not in plane]
+        cross = cross[turn:] + cross[:turn]
+        nth = {}
+        for h in range(NS):
+            src = owner[s][h]
+            k0 = nth.get(src, 0)
+            nth[src] = k0 + 1
+            first, later = [], []
+            for t in cross:
+                u = pair[t]
+                q = [c for c in mate[t] if topo.may_write(c, R[t]) and topo.die(c) == topo.die(src) and c not in brain]
+                q = q[h % len(q)]
+                to = [(R[t], topo.mask(q, R[t]))]
+                if u is not None and u != s:
+                    to.append((R[u], topo.mask(q, R[u]) & ~topo.mask(q, R[t])))
+                if q == src:
+                    key = -2
+                elif u == s:
+                    first.append((q, topo.mask(src, q) & ~topo.mask(q, R[t]), "x%d_%d" % (s, h)))
+                    key = 8 * k0 - 1
+                else:
+                    key = 8 * k0 + len(later)
+                    later.append((q, topo.mask(src, q), "x%d_%d" % (s, h)))
+                fwd.setdefault(q, []).append((key, s, h, to))
+                for d, mk in to:
+                    xin[R.index(d)] += _bits(mk)
+            for t in plane:
+                if t != s and pair[t] is None:
+                    later.append((R[t], topo.mask(src, R[t]), "xin"))
+                    xin[t] += _bits(topo.mask(src, R[t]))
+            for d, mk, sem in first + later:
+                sends.setdefault(src, []).append((s, h, d, mk, sem))
+    _PLAN.update(R=R, chip=chip, brain=brain, owner=owner, sends=sends, fwd=fwd, xin=xin, pair=pair)
+    return _PLAN
+
+
+def rank_program(g, core, T, topo):
+    P = _plan(T, topo)
+    rank = T.rank_of(core)
+    vec, pe, act, syn = g.vector, g.tensor, g.scalar, g.sync
+    QN = [(g, "g"), (vec, "v"), (pe, "t"), (act, "a"), (syn, "s")]
+    evs, sent = [], [0]
+
+    def ev():
+        e = {"s": T.sem["e%d" % len(evs)], "n": 0, "w": []}
+        evs.append(e)
+        return e
+
+    def after(q, *deps):
+        k = [b for a, b in QN if a is q][0]
+        for e in deps:
+            if k not in e["w"]:
+                q.wait_ge(e["s"], e["n"])
+                e["w"].append(k)
+
+    def do(e, ins, n=1):
+        ins.then_inc(e["s"], n)
+        e["n"] += n
+
+    def cols(s, h):
+        a = HEAD + s * BLK + h * SW
+        return T.win[:, a:a + SW]
+
+    def dst(d):
+        rid, pid = topo.addr(d, core)
+        return DstId(rid=rid, pnc=pid)
+
+    def send(out, in_, d, mask, sem):
+        rid, pid = topo.addr(d, core)
+        g.remote_dma(out, in_, T.sem[sem], T.sem.sent, pid, rid, mask)
+        sent[0] += _bits(mask)
+
+    def fused(transfers):
+        g.remote_dma_fused([RemoteDMATransfer(dst_ids=[dst(d) for d, _ in to], dma_engine_mask=mask, remote_sem=T.sem[sem],
+                                              srcs=[a], dsts=[b for _, b in to]) for a, to, mask, sem in transfers],
+                           local_sem=T.sem.sent)
+        sent[0] += sum(_bits(mask) for _, _, mask, _ in transfers)
+
+    if rank is not None:
+        _rank_core(g, core, T, topo, P, (vec, pe, act, syn), rank, ev, after, do, cols, send, fused)
+    elif core in P["brain"]:
+        _brain(g, core, T, topo, P, (vec, pe, act, syn), P["brain"].index(core), ev, after, do, fused)
+    else:
+        got = []
+
+        def arrived(s, h):
+            if (s, h) not in got:
+                n = 4 if core == P["owner"][s][h] else _bits(
+                    [mk for q in P["sends"] for (s2, h2, d, mk, _) in P["sends"][q] if (s2, h2, d) == (s, h, core)][0])
+                g.wait_ge(T.sem["x%d_%d" % (s, h)], n)
+                got.append((s, h))
+        for s, h, d, mask, sem in P["sends"].get(core, []):
+            arrived(s, h)
+            send(cols(s, h), cols(s, h), d, mask, sem)
+        for key, s, h, to in sorted(P["fwd"].get(core, []), key=lambda v: v[:3]):
+            arrived(s, h)
+            fused([(cols(s, h), [(d, cols(s, h))], mask, "xin") for d, mask in to])
+    for e in evs:
+        if not e["w"] and e["n"]:
+            g.wait_ge(e["s"], e["n"])
+    if sent[0]:
+        g.wait_ge(T.sem.sent, sent[0])
+
+
+def _rank_core(g, core, T, topo, P, Q, r, ev, after, do, cols, send, fused):
+    vec, pe, act, syn = Q
+    R, brain = P["R"], P["brain"][r]
+    b0 = HEAD + r * BLK
+    e_e, e_pad = ev(), ev()
+    do(e_pad, vec.memset(T.win[:, 0:HEAD], 0.0))
+    do(e_pad, vec.memset(T.win[:, b0 + HALF:b0 + HALF + 1], 0.0))
+    do(e_pad, vec.memset(T.win[:, b0 + 4097:b0 + BLK], 0.0))
+    e_lw = ev()
+    do(e_lw, vec.memset(T.lw[:], 0.0))
+    do(e_e, syn.dma_start(T.eb[:, 0:32], T.e1[:]), 16)
+    do(e_e, act.dma_start(T.eb[:, 32:64], T.e2[:]), 16)
+    e_x = []
+    for k in range(4):
+        q = (syn, act)[k % 2]
+        e_x.append(ev())
+        after(q, e_pad)
+        a = b0 + 1024 * k + (1 if k >= 2 else 0)
+        do(e_x[k], q.dma_start(T.win[:, a:a + 1024], T.x[:, 1024 * k:1024 * k + 1024]), 16)
+    e_i = ev()
+    do(e_i, g.iota(T.ifq[:], [[1, 128]], 0, 0))
+    do(e_i, g.iota(T.iq[:], [[1, 1]], 0, 1))
+    do(e_i, g.iota(T.cib[:], [[0, 4], [16, 8]], -1, 0))
+    off = topo.mask(core, [c for c in R if topo.same_plane(core, c)][0])
+    after(g, e_e)
+    send(T.eb[:], T.eb[:], brain, topo.mask(core, brain) & off, "ein")
+    full = topo.mask(core, brain)
+    eng = [1 << i for i in range(16) if full >> i & 1]
+    quads = [sum(eng[i:i + 4]) for i in range(0, len(eng), 4)]
+    own = P["owner"][r]
+    for hs, need in ((range(0, 4), e_x[0:3]), (range(4, 8), e_x[2:4])):
+        hs = [h for h in hs if own[h] != core]
+        after(g, *need)
+        fused([(cols(r, h), [(own[h], cols(r, h))], quads[i], "x%d_%d" % (r, h)) for i, h in enumerate(hs)])
+    for s, h, d, mask, sem in P["sends"].get(core, []):
+        send(cols(s, h), cols(s, h), d, mask, sem)
+    tf, ti, kA = T.tf, T.ti, 2 * r
+    hh = kA // 8
+    after(vec, e_i)
+    c1 = ev()
+    do(c1, vec.tensor_scalar(ti[:, 0:1], T.iq[:], 15, None, A.bitwise_and))
+    do(c1, vec.tensor_scalar(ti[:, 1:2], T.iq[:], 4, None, A.arith_shift_right))
+    do(c1, vec.tensor_scalar(T.pmi[:], T.ifq[:], 15, None, A.bitwise_and))
+    do(c1, vec.tensor_copy(tf[:, 0:1], T.iq[:]))
+    after(vec, c1)
+    c2 = ev()
+    do(c2, vec.tensor_copy(tf[:, 1:2], ti[:, 0:1]))
+    do(c2, vec.tensor_copy(tf[:, 2:3], ti[:, 1:2]))
+    do(c2, vec.tensor_scalar(T.d2[:], T.ifq[:], tf[:, 0:1], None, A.subtract))
+    after(vec, c2)
+    c3 = ev()
+    do(c3, vec.tensor_scalar(T.dm[:], T.pmi[:], tf[:, 1:2], None, A.subtract))
+    do(c3, vec.tensor_scalar(tf[:, 3:4], tf[:, 2:3], float(r), None, A.is_equal))
+    do(c3, vec.tensor_scalar(tf[:, 8:16], T.ifq[:, 0:8], tf[:, 2:3], None, A.is_lt))
+    do(c3, vec.tensor_scalar(tf[:, 4:5], tf[:, 2:3], float(BLK), float(HEAD + HALF), A.mult, A.add))
+    for e in range(2):
+        do(c3, vec.tensor_scalar(tf[:, 5 + e:6 + e], tf[:, 0:1], float(16 * ((kA + e) % 8)), None, A.is_equal))
+    do(c3, vec.tensor_scalar(T.ci[:], T.cib[:], tf[:, 1:2], None, A.add))
+    after(vec, c3)
+    c4 = ev()
+    for e in range(2):
+        do(c4, vec.tensor_scalar(T.sel[:, 128 * e:128 * e + 128], T.ifq[:], 0.0, tf[:, 5 + e:6 + e], A.is_ge, A.mult))
+    for k in range(8):
+        do(c4, vec.tensor_scalar(T.mats[:, 128 * k:128 * k + 128], T.d2[:], float(16 * (k - r)), tf[:, 3:4], A.is_equal, A.mult))
+    after(pe, c4)
+    pe.wait_ge(T.sem.cnt2, 8 * _bits(off))
+    p1 = ev()
+    for e in range(2):
+        do(p1, pe.matmul(T.pa[:, 32 * e:32 * e + 32], T.sel[:, 128 * e:128 * e + 128], T.cc[:], True, True))
+    after(vec, p1)
+    s1 = ev()
+    for e in range(2):
+        nn, mm = T.pa[:, 32 * e + hh:32 * e + 32:4], T.pa[:, 32 * e + 2 + hh:32 * e + 32:4]
+        do(s1, vec.tensor_tensor(T.tm[:, 16 * e:16 * e + 8], nn, tf[:, 8:16], A.mult))
+        do(s1, vec.tensor_tensor(T.tm[:, 16 * e + 8:16 * e + 16], mm, tf[:, 8:16], A.mult))
+        do(s1, vec.tensor_reduce(tf[:, 16 + e:17 + e], nn, AxisListType.X, A.add))
+    after(vec, s1)
+    s2 = ev()
+    for e in range(2):
+        do(s2, vec.tensor_reduce(tf[:, 20 + e:21 + e], T.tm[:, 16 * e:16 * e + 8], AxisListType.X, A.add))
+        do(s2, vec.tensor_reduce(tf[:, 18 + e:19 + e], T.tm[:, 16 * e + 8:16 * e + 16], AxisListType.X, A.add))
+    do(s2, vec.tensor_scalar(tf[:, 24:26], tf[:, 16:18], 1920.0, None, A.min))
+    after(vec, s2)
+    s3 = ev()
+    do(s3, vec.tensor_tensor(tf[:, 22:24], tf[:, 24:26], tf[:, 18:20], A.add))
+    after(vec, s3)
+    s4 = ev()
+    do(s4, vec.tensor_copy(T.si[:, 0:4], tf[:, 20:24]))
+    after(vec, s4)
+    s5 = ev()
+    do(s5, vec.tensor_scalar(T.si[:, 4:8], T.si[:, 0:4], 4, None, A.arith_shift_right))
+    do(s5, vec.tensor_scalar(T.si[:, 8:12], T.si[:, 0:4], 15, None, A.bitwise_and))
+    after(vec, s5)
+    s6 = ev()
+    do(s6, vec.tensor_copy(tf[:, 26:30], T.si[:, 4:8]))
+    do(s6, vec.tensor_copy(tf[:, 30:34], T.si[:, 8:12]))
+    do(s6, vec.tensor_scalar(tf[:, 34:38], T.si[:, 8:12], -16.0, None, A.add))
+    after(vec, s6)
+    s7, s8 = ev(), ev()
+    for l in range(4):
+        do(s7, vec.tensor_scalar(T.cj[:, 8 * l:8 * l + 8], T.ci[:, 8 * l:8 * l + 8], tf[:, 26 + l:27 + l], -1.0, A.subtract, A.max))
+    for l in range(4):
+        for ab in range(2):
+            c, k = 30 + 4 * ab + l, 2 * (2 * l + ab)
+            do(s8, vec.tensor_scalar(T.rot[:, 128 * k:128 * k + 128], T.dm[:], tf[:, c:c + 1], None, A.is_equal))
+            do(s8, vec.tensor_scalar(T.rot[:, 128 * k + 128:128 * k + 256], T.dm[:], tf[:, c:c + 1], tf[:, 4:5], A.is_equal, A.mult))
+    after(vec, s7)
+    s9 = ev()
+    for l in range(4):
+        do(s9, vec.tensor_scalar(T.ix[:, 8 * l:8 * l + 8], T.cj[:, 8 * l:8 * l + 8], 32.0, float(34 * l + 1), A.min, A.add))
+    pe.wait_ge(T.sem.lists, 8 * _bits(off))
+    p2 = ev()
+    for k in range(8):
+        i = pe.matmul(T.pb[:, 0:128], T.mats[:, 128 * k:128 * k + 128], T.ls[:, 128 * k:128 * k + 128], k == 0, k == 7)
+    do(p2, i)
+    after(vec, p2, e_lw)
+    w1 = ev()
+    for l in range(4):
+        do(w1, vec.tensor_copy(T.lw[:, 34 * l + 1:34 * l + 33], T.pb[:, 32 * l:32 * l + 32]))
+    after(vec, w1, s9)
+    w2 = ev()
+    do(w2, vec.tensor_copy(T.gg[:], T.lw[:, 0:136].indirect(T.ix[:, 0:32])))
+    after(vec, w2)
+    w3 = ev()
+    do(w3, vec.tensor_scalar(T.gp[:], T.gg[:], 0.0, None, A.not_equal))
+    pw = [ev(), ev()]
+    bank = (T.pc, T.pd)
+    after(pe, s8, w2)
+    for k, src in ((0, T.gg), (1, T.gp)):
+        if k:
+            after(pe, w3)
+        for e in range(2):
+            for l in (e, 2 + e):
+                for ab in range(2):
+                    c = 128 * (2 * (2 * l + ab) + k)
+                    i = pe.matmul(bank[e][:, 0:120], T.rot[:, c:c + 128], src[:, 128 * l + 1 - ab:128 * l + 121 - ab],
+                                  k == 0 and l == e and ab == 0, k == 1 and l == 2 + e and ab == 1)
+            if k:
+                do(pw[e], i)
+    wo = [ev(), ev()]
+    for e in range(2):
+        after(vec, pw[e])
+        do(wo[e], vec.tensor_copy(T.ofs[:, 120 * e:120 * e + 120], bank[e][:, 0:120]))
+    for q, e in ((vec, 0), (act, 1)):
+        q.wait_ge(T.sem.xin, P["xin"][r])
+        after(q, e_pad, wo[e], *e_x)
+    stores = []
+    for k in range(2):
+        for e in range(2):
+            a, o = 1920 * e + 960 * k, 120 * e + 60 * k
+            y = ev()
+            win = T.win[:, 0:WIN].indirect(T.ofs[:, o:o + 60])
+            if e == 0:
+                do(y, vec.tensor_copy(T.yo[:, a:a + 960], win))
+            else:
+                do(y, act.activation(T.yo[:, a:a + 960], win, AF.Copy))
+            stores.append((y, a))
+    e_y = ev()
+    for y, a in stores:
+        after(syn, y)
+        do(e_y, syn.dma_start(T.y[:, a:a + 960], T.yo[:, a:a + 960]), 16)
+    after(syn, e_y)
+
+
+def _brain(g, core, T, topo, P, Q, r, ev, after, do, fused):
+    vec, pe, act, _ = Q
+    R, brains = P["R"], P["brain"]
+    tf, ti = T.tf, T.ti
+    off = topo.mask(core, [c for c in R if c != R[r]][0])
+    e_i = ev()
+    do(e_i, g.iota(T.ifq[:], [[1, 128]], 0, 0))
+    do(e_i, g.iota(T.iq[:], [[1, 1]], 0, 1))
+    do(e_i, g.iota(T.val[:], [[2049, 2], [1, 16]], -2048, 16, allow_small_or_imprecise_dtypes=True))
+    after(vec, e_i)
+    c1 = ev()
+    do(c1, vec.tensor_copy(tf[:, 0:1], T.iq[:]))
+    for c, sc, op in ((0, 15, A.bitwise_and), (1, 4, A.arith_shift_right), (2, 7, A.bitwise_and), (3, 3, A.arith_shift_right)):
+        do(c1, vec.tensor_scalar(ti[:, c:c + 1], T.iq[:], sc, None, op))
+    do(c1, vec.tensor_scalar(T.pmi[:], T.ifq[:], 15, None, A.bitwise_and))
+    do(c1, vec.tensor_scalar(T.gfi[:], T.ifq[:], 4, None, A.arith_shift_right))
+    do(c1, vec.tensor_copy(T.iot[:], T.ifq[:]))
+    after(vec, c1)
+    c2 = ev()
+    do(c2, vec.tensor_copy(tf[:, 1:5], ti[:, 0:4]))
+    do(c2, vec.tensor_scalar(T.d2[:], T.iot[:], tf[:, 0:1], None, A.subtract))
+    after(vec, c2)
+    c3 = ev()
+    for k, add in ((8, 8.0), (9, 64.0), (10, 72.0)):
+        do(c3, vec.tensor_scalar(tf[:, k:k + 1], tf[:, 2:3], add, None, A.add))
+    for k in range(8):
+        do(c3, vec.tensor_scalar(tf[:, 16 + k:17 + k], tf[:, 3:4], float(k), None, A.is_equal))
+    do(c3, vec.tensor_scalar(T.bo[:], T.gfi[:], tf[:, 2:3], None, A.is_equal))
+    do(c3, vec.tensor_scalar(T.gs[:], T.pmi[:], tf[:, 1:2], 64.0, A.is_equal, A.mult))
+    do(c3, vec.tensor_scalar(T.gt[:], T.ifq[:, 0:16], tf[:, 1:2], None, A.is_equal))
+    do(c3, vec.tensor_scalar(T.idb[:], T.d2[:], 0.0, None, A.is_equal))
+    do(c3, vec.tensor_scalar(T.idf[:], T.d2[:], 0.0, 2049.0, A.is_equal, A.mult))
+    do(c3, vec.tensor_scalar(T.u1[:], T.d2[:], 0.0, -1.0, A.is_le, A.mult))
+    after(vec, c3)
+    c4 = ev()
+    for k in range(8):
+        do(c4, vec.tensor_scalar(T.mats[:, 128 * k:128 * k + 128], T.pmi[:], tf[:, 4:5], tf[:, 16 + k:17 + k], A.is_equal, A.mult))
+    do(c4, vec.tensor_tensor(T.u1[:], T.u1[:], T.bo[:], A.mult))
+    after(vec, c4)
+    c7 = ev()
+    do(c7, vec.tensor_tensor(T.up[:], T.u1[:], T.idf[:], A.add))
+    vec.wait_ge(T.sem.ein, _bits(off))
+    v0 = ev()
+    do(v0, vec.tensor_copy(T.ef[:], T.eb[:]))
+    after(pe, c4, v0)
+    t0 = ev()
+    for w in range(2):
+        for k in range(8):
+            a = 256 * w + 32 * k
+            do(t0, pe.matmul(T.pa[:, a:a + 32], T.mats[:, 128 * k:128 * k + 128], T.ef[:, 32 * w:32 * w + 32], True, True))
+    after(vec, t0)
+    v1 = ev()
+    for h in range(2):
+        do(v1, vec.tensor_scalar(T.mm[:, 256 * h:256 * h + 256], T.pa[:, 0:256], tf[:, (2, 8)[h]:(3, 9)[h]], None, A.is_equal))
+    after(vec, v1)
+    v2 = ev()
+    for h in range(2):
+        a = slice(256 * h, 256 * h + 256)
+        do(v2, vec.tensor_tensor_scan(T.cu[:, a], T.mm[:, a], T.mm[:, a], 0.0, A.add, A.max))
+    after(pe, c7, v2)
+    t1, t2 = ev(), ev()
+    for h in range(2):
+        do(t1, pe.matmul(T.pe[:, h:h + 1], T.bo[:], T.cu[:, 256 * h + 255:256 * h + 256], True, True))
+    pe.matmul(T.pb[:], T.bo[:], T.cu[:], True, False)
+    do(t2, pe.matmul(T.pb[:], T.up[:], T.mm[:], False, True))
+    after(vec, t1)
+    v3 = ev()
+    do(v3, vec.tensor_copy(T.cs[:, 0:2], T.pe[:, 0:2]))
+    later = range(r + 1, len(R))
+    after(g, v3)
+    if later:
+        fused([(T.cs[:, 0:2], [(brains[k], T.cn[:, 2 * r:2 * r + 2]) for k in later], off, "cnt1")])
+    after(act, v1, t0)
+    a1 = ev()
+    do(a1, act.activation(T.er[:], T.pa[:], AF.Copy))
+    after(pe, a1)
+    t3, t4 = ev(), ev()
+    for w in range(2):
+        for cb in range(2):
+            do(t3, pe.matmul(T.pf[:, 32 * w + 16 * cb:32 * w + 16 * cb + 16], T.er[:, 256 * w + 128 * cb:256 * w + 128 * cb + 128],
+                             T.idb[:, 0:16], True, True))
+    pe.matmul(T.pc[:, 0:256], T.idb[:], T.er[:, 256:512], True, False)
+    after(vec, t2)
+    v4 = ev()
+    do(v4, vec.tensor_scalar(T.v1[:], T.pb[:], -2048.0, 0.0, A.add, A.max))
+
+    def per_token(bank, a, src, e):
+        for cb in range(2):
+            for h in range(2):
+                i = pe.matmul(bank[:, a + 16 * cb:a + 16 * cb + 16], src[:, 256 * h + 128 * cb:256 * h + 128 * cb + 128],
+                              T.gt[:], h == 0, h == 1)
+            do(e, i)
+    after(pe, v4)
+    per_token(T.pf, 64, T.v1, t4)
+    ki, kf = T.ki, T.kf
+
+    def c(k):
+        return slice(32 * k, 32 * k + 32)
+    after(vec, t3, t4)
+    k1 = ev()
+    do(k1, vec.tensor_copy(ki[:, 0:64], T.pf[:, 0:64]))
+    do(k1, vec.tensor_scalar(ki[:, c(2)], T.pf[:, 64:96], -1.0, None, A.add))
+    after(vec, k1)
+    k2 = ev()
+    do(k2, vec.tensor_scalar(ki[:, 96:160], ki[:, 0:64], 1, None, A.arith_shift_right))
+    do(k2, vec.tensor_scalar(ki[:, 160:224], ki[:, 0:64], 1, None, A.bitwise_and))
+    do(k2, vec.tensor_scalar(ki[:, c(7)], ki[:, c(2)], 15, None, A.bitwise_and))
+    do(k2, vec.tensor_scalar(ki[:, c(8)], ki[:, c(2)], 4, None, A.arith_shift_right))
+    after(vec, k2)
+    k3 = ev()
+    do(k3, vec.tensor_scalar(kf[:, 0:64], ki[:, 96:160], 16.0, None, A.mult))
+    do(k3, vec.tensor_scalar(kf[:, c(2)], ki[:, c(5)], 32.0, None, A.mult))
+    do(k3, vec.tensor_scalar(kf[:, c(3)], ki[:, c(6)], 32.0, 64.0, A.mult, A.add))
+    after(vec, k3)
+    k4 = ev()
+    do(k4, vec.tensor_tensor(kf[:, c(4)], kf[:, c(0)], ki[:, c(7)], A.add))
+    do(k4, vec.tensor_tensor(kf[:, c(5)], kf[:, c(2)], ki[:, c(8)], A.add))
+    after(vec, k4)
+    k5 = ev()
+    do(k5, vec.tensor_tensor(kf[:, c(6)], kf[:, c(1)], kf[:, c(4)], A.subtract))
+    do(k5, vec.tensor_tensor(kf[:, c(7)], kf[:, c(3)], kf[:, c(5)], A.subtract))
+    if r:
+        vec.wait_ge(T.sem.cnt1, r * _bits(off))
+        f1 = ev()
+        for h in range(2):
+            do(f1, vec.tensor_reduce(tf[:, 24 + h:25 + h], T.cn[:, h:2 * r:2], AxisListType.X, A.add, negate=True))
+        after(vec, f1)
+        f2 = ev()
+        do(f2, vec.tensor_scalar(tf[:, 26:28], tf[:, 24:26], 1920.0 + 2049.0, 2049.0, A.add, A.max))
+        after(vec, f2)
+    f3 = ev()
+    for h in range(2):
+        a = slice(256 * h, 256 * h + 256)
+        do(f3, vec.tensor_scalar(T.ff[:, a], T.pb[:, a], tf[:, 26 + h:27 + h] if r else 3969.0, None, A.is_ge))
+    after(pe, f3)
+    t5, t6 = ev(), ev()
+    pe.matmul(T.pc[:, 0:256], T.gs[:], T.ff[:, 0:256], False, False)
+    do(t5, pe.matmul(T.pc[:, 0:256], T.gs[:], T.ff[:, 256:512], False, True))
+    per_token(T.ph, 0, T.ff, t6)
+    after(vec, t5)
+    f4 = ev()
+    for h in range(2):
+        do(f4, vec.tensor_scalar(T.m2[:, 256 * h:256 * h + 256], T.pc[:, 0:256], tf[:, 9 + h:10 + h], None, A.is_equal))
+    after(vec, f4)
+    f5 = ev()
+    for h in range(2):
+        a = slice(256 * h, 256 * h + 256)
+        do(f5, vec.tensor_tensor_scan(T.c2[:, a], T.m2[:, a], T.m2[:, a], 0.0, A.add, A.max))
+    after(pe, f5)
+    t7, t8 = ev(), ev()
+    pe.matmul(T.pd[:], T.bo[:], T.c2[:], True, False)
+    do(t8, pe.matmul(T.pd[:], T.up[:], T.m2[:], False, True))
+    for h in range(2):
+        do(t7, pe.matmul(T.pe[:, 2 + h:3 + h], T.bo[:], T.c2[:, 256 * h + 255:256 * h + 256], True, True))
+    after(vec, t6, k5)
+    k6 = ev()
+    do(k6, vec.tensor_tensor(kf[:, c(8)], kf[:, c(6)], T.ph[:, 0:32], A.mult))
+    do(k6, vec.tensor_tensor(kf[:, c(9)], kf[:, c(7)], T.ph[:, 0:32], A.mult))
+    after(vec, k6)
+    k7 = ev()
+    do(k7, vec.tensor_tensor(kf[:, c(10)], kf[:, c(8)], kf[:, c(4)], A.add))
+    do(k7, vec.tensor_tensor(kf[:, c(11)], kf[:, c(9)], kf[:, c(5)], A.add))
+    after(vec, t8)
+    f6 = ev()
+    do(f6, vec.tensor_scalar(T.v2[:], T.pd[:], -2048.0, 0.0, A.add, A.max))
+    after(vec, t7)
+    f7 = ev()
+    do(f7, vec.tensor_copy(T.cs[:, 2:4], T.pe[:, 2:4]))
+    after(pe, f6, k6)
+    t9 = ev()
+    per_token(T.ph, 32, T.v2, t9)
+    after(g, f7)
+    fused([(T.cs[:, 0:4], [(d, T.cc[:, 4 * r:4 * r + 4]) for d in R], off, "cnt2")])
+    after(vec, t9)
+    k8 = ev()
+    do(k8, vec.tensor_scalar(ki[:, c(9)], T.ph[:, 32:64], -1.0, 0.0, A.add, A.max))
+    after(vec, k8)
+    k9 = ev()
+    do(k9, vec.tensor_scalar(ki[:, c(10)], ki[:, c(9)], 15, None, A.bitwise_and))
+    do(k9, vec.tensor_scalar(ki[:, c(11)], ki[:, c(9)], 4, None, A.arith_shift_right))
+    after(vec, k9, k7)
+    k10 = ev()
+    do(k10, vec.tensor_tensor(kf[:, c(12)], kf[:, c(10)], ki[:, c(10)], A.add))
+    do(k10, vec.tensor_tensor(kf[:, c(13)], kf[:, c(11)], ki[:, c(11)], A.add))
+    after(vec, k10)
+    for b0 in range(0, 32, 4):
+        o = ev()
+        for b in range(b0, b0 + 4):
+            a = slice(128 * b, 128 * b + 128)
+            do(o, vec.tensor_scalar(T.oh[:, a], T.iot[:], kf[:, 384 + b:385 + b], None, A.is_equal))
+            do(o, vec.tensor_scalar(T.ol[:, a], T.iot[:], kf[:, 416 + b:417 + b], T.val[:, b:b + 1], A.is_equal, A.mult))
+        after(pe, o)
+        for b in range(b0, b0 + 4):
+            a = slice(128 * b, 128 * b + 128)
+            i = pe.matmul(T.pg[:, 0:128], T.oh[:, a], T.ol[:, a], b == 0, b == 31)
+    t10 = ev()
+    do(t10, i)
+    after(vec, t10)
+    l1 = ev()
+    do(l1, vec.tensor_copy(T.lf[:], T.pg[:, 0:128]))
+    after(g, l1)
+    fused([(T.lf[:], [(d, T.ls[:, 128 * r:128 * r + 128]) for d in R], off, "lists")])

@@ -1,42 +1,56 @@
 from concourse.bass import DstId, RemoteDMATransfer
 from concourse.mybir import AluOpType as A, AxisListType, ActivationFunctionType as AF
 
-NS, SW = 8, 514
-BLK, HEAD = NS * SW, 16
-HALF = 2048
-WIN = HEAD + 8 * BLK
-NEV = 72
+N, CAP, CAPP = 8, 1920, 512
+FULL = CAP // CAPP
+BW = 2 * CAPP
+NB = N + N - FULL
+ZERO = NB * BW
+WIN = ZERO + 16
+NS, SR = 8, 16
+BIG, B8 = 2049, 1024
+WS = 1664
+NEV = 110
 
+F16, F32, I32, U16, BF = "float16", "float32", "int32", "uint16", "bfloat16"
 SCRATCH = {
-    "win": ("sbuf", [128, WIN], "bfloat16"),
-    "yo": ("sbuf", [128, 3840], "bfloat16"),
-    "eb": ("sbuf", [128, 64], "int32"),
-    "ifq": ("sbuf", [128, 128], "int32"), "iq": ("sbuf", [128, 1], "int32"), "cib": ("sbuf", [128, 32], "int32"),
-    "ti": ("sbuf", [128, 8], "int32"), "tf": ("sbuf", [128, 48], "float32"), "pmi": ("sbuf", [128, 128], "int32"),
-    "gfi": ("sbuf", [128, 128], "int32"),
-    "d2": ("sbuf", [128, 128], "float16"), "dm": ("sbuf", [128, 128], "float16"),
-    "mats": ("sbuf", [128, 1024], "float16"), "rot": ("sbuf", [128, 2048], "float16"),
-    "sel": ("sbuf", [128, 256], "float32"),
-    "ci": ("sbuf", [128, 32], "float32"), "cj": ("sbuf", [128, 32], "float32"), "ix": ("sbuf", [128, 32], "uint16"),
-    "si": ("sbuf", [128, 12], "int32"), "tm": ("sbuf", [128, 32], "float32"),
-    "cc": ("sbuf", [128, 32], "float32"), "cn": ("sbuf", [128, 16], "float32"), "cs": ("sbuf", [128, 4], "float32"),
-    "ls": ("sbuf", [128, 1024], "float16"), "lw": ("sbuf", [128, 136], "float32"),
-    "gg": ("sbuf", [128, 512], "float16"), "gp": ("sbuf", [128, 512], "float16"),
-    "ofs": ("sbuf", [128, 240], "uint16"),
-    "ef": ("sbuf", [128, 64], "float16"), "er": ("sbuf", [128, 512], "bfloat16"),
-    "bo": ("sbuf", [128, 128], "float16"), "up": ("sbuf", [128, 128], "float16"), "u1": ("sbuf", [128, 128], "float16"),
-    "gs": ("sbuf", [128, 128], "float16"), "gt": ("sbuf", [128, 16], "float16"), "idb": ("sbuf", [128, 128], "bfloat16"),
-    "idf": ("sbuf", [128, 128], "float32"), "iot": ("sbuf", [128, 128], "float16"), "val": ("sbuf", [128, 32], "float32"),
-    "mm": ("sbuf", [128, 512], "float16"), "cu": ("sbuf", [128, 512], "float16"), "v1": ("sbuf", [128, 512], "float16"),
-    "ff": ("sbuf", [128, 512], "float16"), "m2": ("sbuf", [128, 512], "float16"), "c2": ("sbuf", [128, 512], "float16"),
-    "v2": ("sbuf", [128, 512], "float16"),
-    "ki": ("sbuf", [128, 512], "int32"), "kf": ("sbuf", [128, 512], "float32"),
-    "oh": ("sbuf", [128, 4096], "float16"), "ol": ("sbuf", [128, 4096], "float16"), "lf": ("sbuf", [128, 128], "float16"),
+    "ed1": ("dram", [128, 32], I32), "ed2": ("dram", [128, 32], I32),
+    "cd": ("dram", [128, 2], F16), "cin": ("dram", [8, 128, 2], F16), "xd": ("dram", [NS, 128, 512], BF),
+    "xb": ("sbuf", [128, 4096], BF), "win": ("sbuf", [128, WIN], BF), "yo": ("sbuf", [128, 2 * CAP], BF),
+    "ob1": ("sbuf", [128, BW], BF), "ob2": ("sbuf", [128, BW], BF),
+    "eb": ("sbuf", [128, 256], I32), "e8": ("sbuf", [128, 64], I32), "ef": ("sbuf", [128, 256], F16),
+    "iq": ("sbuf", [128, 1], I32), "ti": ("sbuf", [128, 4], I32), "tf": ("sbuf", [128, 64], F32),
+    "em": ("sbuf", [128, 144], BF), "rz": ("sbuf", [128, 64], BF),
+    "mm": ("sbuf", [128, 512], F16), "cu": ("sbuf", [128, 512], F16), "ff": ("sbuf", [128, 512], F16),
+    "cs": ("sbuf", [128, 256], F16), "cl": ("sbuf", [128, 256], F16), "thr": ("sbuf", [128, 2], F32),
+    "cx": ("sbuf", [128, 4], F32), "cc": ("sbuf", [128, 32], F32), "e2m": ("sbuf", [128, 64], F16),
+    "pr": ("sbuf", [128, 128], F32), "aa": ("sbuf", [128, 480], F16), "of": ("sbuf", [128, 240], U16),
+    "qw1": ("sbuf", [128, WS], BF), "qw2": ("sbuf", [128, WS], BF),
 }
+_AT = {}
+
+
+def _share(buf, dtype, parts):
+    at = 0
+    for name, width in parts:
+        _AT[name] = (buf, at, width)
+        at += width
+    SCRATCH[buf] = ("sbuf", [128, at], dtype)
+
+
+_share("fx", F32, [("fi", 128), ("fm", 128), ("fd", 128), ("f8", 128), ("gx", 136), ("um", 144), ("dump", 32), ("pv", 120),
+                   ("jj", 16), ("mk", 64), ("sc", 16), ("t2", 128)])
+_share("dq", BF, [("da", 512), ("db", 512), ("dc", 512), ("de", 512), ("dd", 512)])
+_share("kk", F16, [("rr", 128), ("bo", 128), ("up", 128), ("bo8", 128), ("pre8", 128), ("ua", 128), ("ub", 128), ("one", 128),
+                   ("s8", 128), ("ge", 136), ("t1", 128), ("t3", 128), ("t4", 128), ("t5", 128), ("t6", 128), ("t7", 128),
+                   ("pw", 120), ("pg0", 120), ("neg", 8)])
+for _k in "12":
+    _share("qf" + _k, F32, [("dx" + _k, 32), ("dy" + _k, 32), ("z" + _k, 64), ("u" + _k, 32), ("v" + _k, 32)])
+    _share("qh" + _k, F16, [("m" + _k, 64), ("c" + _k, 64), ("ms" + _k, 32)])
+    _share("qo" + _k, U16, [("o" + _k, 32), ("l" + _k, 64)])
 for _n in "abcdefgh":
-    SCRATCH["p" + _n] = ("psum", [128, 512], "float32")
-SEMAPHORES = (["x%d_%d" % (s, h) for s in range(8) for h in range(NS)] + ["e%d" % i for i in range(NEV)]
-              + ["xin", "ein", "cnt1", "cnt2", "lists", "sent"])
+    SCRATCH["p" + _n] = ("psum", [128, 512], F32)
+SEMAPHORES = ["e%d" % i for i in range(NEV)] + ["ein1", "ein2", "cin", "ccs", "wins", "sent"] + ["xs%d" % i for i in range(NS)]
 
 _PLAN = {}
 
@@ -45,68 +59,101 @@ def _bits(m):
     return bin(m).count("1")
 
 
+def _engines(m):
+    return [1 << i for i in range(16) if m >> i & 1]
+
+
+def _perms(v):
+    return [[]] if not v else [[a] + p for i, a in enumerate(v) for p in _perms(v[:i] + v[i + 1:])]
+
+
 def _plan(T, topo):
     if _PLAN:
         return _PLAN
-    R, n = list(T.cores), len(T.cores)
-    everyone = range(256)
-    chip = [[c for c in everyone if topo.host(c) == topo.host(R[r]) and topo.chip(c) == topo.chip(R[r])] for r in range(n)]
-    mate = [[c for c in everyone if topo.mates(c, R[r])] for r in range(n)]
-    pair = [([u for u in range(n) if R[u] in mate[r]] + [None])[0] for r in range(n)]
-    near = [[c for c in chip[r] if topo.die(c) == topo.die(R[r]) and c != R[r]] for r in range(n)]
-    brain = [[c for c in near[r] if topo.may_write(c, mate[r][0])][0] for r in range(n)]
-    owner = []
-    for r in range(n):
-        p = [c for c in near[r] if not topo.may_write(c, mate[r][0])][0]
-        m = [c for c in near[r] if c not in (p, brain[r])][0]
-        far = [c for c in chip[r] if topo.die(c) != topo.die(R[r])]
-        owner.append(([p, p, R[r], R[r]] if pair[r] is not None else [p, p, m, R[r]]) + far)
-    sends, fwd, xin = {}, {}, [0] * n
-    for s in range(n):
-        plane = [t for t in range(n) if t == s or topo.same_plane(R[s], R[t])]
-        turn = plane.index(s)
-        cross = [t for t in range(n) if t not in plane]
-        cross = cross[turn:] + cross[:turn]
-        nth = {}
-        for h in range(NS):
-            src = owner[s][h]
-            k0 = nth.get(src, 0)
-            nth[src] = k0 + 1
-            first, later = [], []
-            for t in cross:
-                u = pair[t]
-                q = [c for c in mate[t] if topo.may_write(c, R[t]) and topo.die(c) == topo.die(src) and c not in brain]
-                q = q[h % len(q)]
-                to = [(R[t], topo.mask(q, R[t]))]
-                if u is not None and u != s:
-                    to.append((R[u], topo.mask(q, R[u]) & ~topo.mask(q, R[t])))
-                if q == src:
-                    key = -2
-                elif u == s:
-                    first.append((q, topo.mask(src, q) & ~topo.mask(q, R[t]), "x%d_%d" % (s, h)))
-                    key = 8 * k0 - 1
-                else:
-                    key = 8 * k0 + len(later)
-                    later.append((q, topo.mask(src, q), "x%d_%d" % (s, h)))
-                fwd.setdefault(q, []).append((key, s, h, to))
-                for d, mk in to:
-                    xin[R.index(d)] += _bits(mk)
-            for t in plane:
-                if t != s and pair[t] is None:
-                    later.append((R[t], topo.mask(src, R[t]), "xin"))
-                    xin[t] += _bits(topo.mask(src, R[t]))
-            for d, mk, sem in first + later:
-                sends.setdefault(src, []).append((s, h, d, mk, sem))
-    _PLAN.update(R=R, chip=chip, brain=brain, owner=owner, sends=sends, fwd=fwd, xin=xin, pair=pair)
+    R, everyone = list(T.cores), range(256)
+
+    def place(c):
+        return (topo.host(c), topo.chip(c))
+    chip = [[c for c in everyone if place(c) == place(R[r])] for r in range(N)]
+    mate = [[c for c in everyone if topo.mates(c, R[r])][0] for r in range(N)]
+    helpers = [[c for c in chip[r] if c != R[r]] for r in range(N)]
+    cross, plain = [], []
+    for r in range(N):
+        cross.append([t for t in range(N) if t != r and not topo.same_plane(R[r], R[t])])
+        plain.append([t for t in range(N) if topo.same_plane(R[r], R[t])])
+    owners = [[c for c in helpers[r] if topo.may_write(c, mate[r])][:len(cross[r])] for r in range(N)]
+    others = [[c for c in helpers[r] if c not in owners[r]][:len(plain[r])] for r in range(N)]
+
+    def links(r, c, t):
+        d = topo.die(c)
+        if t in cross[r]:
+            if topo.mates(R[r], R[t]):
+                return [("mate", place(R[r]), d)]
+            return [("mate", place(R[r]), d), ("out", place(mate[r]), d), ("in", place(R[t]), d)]
+        return [("out", place(R[r]), d), ("in", place(R[t]), d)]
+    pick = [(list(cross[r]), list(plain[r])) for r in range(N)]
+
+    def uses(r, p):
+        w = 2 if r >= FULL else 1
+        return [(k, w) for c, t in list(zip(owners[r], p[0])) + list(zip(others[r], p[1])) for k in links(r, c, t)]
+    for _ in range(3):
+        for r in range(N):
+            load = {}
+            for s in range(N):
+                if s != r:
+                    for k, w in uses(s, pick[s]):
+                        load[k] = load.get(k, 0) + w
+            best = None
+            for pa in _perms(cross[r]):
+                for pb in _perms(plain[r]):
+                    mine = {}
+                    for k, w in uses(r, (pa, pb)):
+                        mine[k] = mine.get(k, 0) + w
+                    cost = sum((load.get(k, 0) + w) ** 2 - load.get(k, 0) ** 2 for k, w in mine.items())
+                    if best is None or cost < best[0]:
+                        best = (cost, (pa, pb))
+            pick[r] = best[1]
+    role = {}
+    for r in range(N):
+        role[R[r]] = (r, r)
+        for c, t in list(zip(owners[r], pick[r][0])) + list(zip(others[r], pick[r][1])):
+            role[c] = (r, t)
+    cnt = {}
+    for r in range(N):
+        later = [s for s in range(r + 1, N) if s >= FULL]
+        for s in sorted(later, key=lambda t: t in plain[r]):
+            for d in chip[s]:
+                able = [c for c in helpers[r] if topo.may_write(c, d)]
+                c = min(able, key=lambda v: len(cnt.get(v, [])))
+                cnt.setdefault(c, []).append(d)
+    _PLAN.update(R=R, helpers=helpers, role=role, cnt=cnt)
     return _PLAN
+
+
+def _arrivals(P, topo, t, times=None):
+    return sum(_bits(topo.mask(c, P["R"][t])) * (times[r] if times else 1)
+               for c, (r, d) in P["role"].items() if d == t and c != P["R"][t])
 
 
 def rank_program(g, core, T, topo):
     P = _plan(T, topo)
-    rank = T.rank_of(core)
+    if core not in P["role"]:
+        return
+    R = P["R"]
+    r, d = P["role"][core]
+    home = core == R[r]
+    helpers = P["helpers"][r]
+    rest = [c for c in helpers if c != core]
+    second = r >= FULL
+    todo = P["cnt"].get(core, [])
+    counting = todo or second
     vec, pe, act, syn = g.vector, g.tensor, g.scalar, g.sync
     QN = [(g, "g"), (vec, "v"), (pe, "t"), (act, "a"), (syn, "s")]
     evs, sent = [], [0]
+
+    def C(name, a=0, b=None, step=1, rows=128):
+        buf, at, width = _AT[name]
+        return T[buf][0:rows, at + a:at + (width if b is None else b):step]
 
     def ev():
         e = {"s": T.sem["e%d" % len(evs)], "n": 0, "w": []}
@@ -124,414 +171,371 @@ def rank_program(g, core, T, topo):
         ins.then_inc(e["s"], n)
         e["n"] += n
 
-    def cols(s, h):
-        a = HEAD + s * BLK + h * SW
-        return T.win[:, a:a + SW]
+    def one(q, deps, make, n=1):
+        after(q, *deps)
+        e = ev()
+        do(e, make(), n)
+        return e
 
-    def dst(d):
-        rid, pid = topo.addr(d, core)
+    def issued():
+        e = ev()
+        g.sem_inc(e["s"], 1)
+        e["n"] += 1
+        return e
+
+    def dst(c):
+        rid, pid = topo.addr(c, core)
         return DstId(rid=rid, pnc=pid)
 
-    def send(out, in_, d, mask, sem):
-        rid, pid = topo.addr(d, core)
-        g.remote_dma(out, in_, T.sem[sem], T.sem.sent, pid, rid, mask)
-        sent[0] += _bits(mask)
-
     def fused(transfers):
-        g.remote_dma_fused([RemoteDMATransfer(dst_ids=[dst(d) for d, _ in to], dma_engine_mask=mask, remote_sem=T.sem[sem],
+        g.remote_dma_fused([RemoteDMATransfer(dst_ids=[dst(c) for c, _ in to], dma_engine_mask=mask, remote_sem=T.sem[sem],
                                               srcs=[a], dsts=[b for _, b in to]) for a, to, mask, sem in transfers],
                            local_sem=T.sem.sent)
         sent[0] += sum(_bits(mask) for _, _, mask, _ in transfers)
 
-    if rank is not None:
-        _rank_core(g, core, T, topo, P, (vec, pe, act, syn), rank, ev, after, do, cols, send, fused)
-    elif core in P["brain"]:
-        _brain(g, core, T, topo, P, (vec, pe, act, syn), P["brain"].index(core), ev, after, do, fused)
-    else:
-        got = []
+    tf, ti = T.tf, T.ti
+    ts, tt, tc = vec.tensor_scalar, vec.tensor_tensor, vec.tensor_copy
+    imp = {"allow_small_or_imprecise_dtypes": True}
 
-        def arrived(s, h):
-            if (s, h) not in got:
-                n = 4 if core == P["owner"][s][h] else _bits(
-                    [mk for q in P["sends"] for (s2, h2, d, mk, _) in P["sends"][q] if (s2, h2, d) == (s, h, core)][0])
-                g.wait_ge(T.sem["x%d_%d" % (s, h)], n)
-                got.append((s, h))
-        for s, h, d, mask, sem in P["sends"].get(core, []):
-            arrived(s, h)
-            send(cols(s, h), cols(s, h), d, mask, sem)
-        for key, s, h, to in sorted(P["fwd"].get(core, []), key=lambda v: v[:3]):
-            arrived(s, h)
-            fused([(cols(s, h), [(d, cols(s, h))], mask, "xin") for d, mask in to])
+    if home:
+        e_d1 = one(syn, [], lambda: syn.dma_start(T.ed1[:], T.e1[:]), 16)
+        e_d2 = one(act, [], lambda: act.dma_start(T.ed2[:], T.e2[:]), 16)
+        s1, s2 = T.e1, T.e2
+    else:
+        syn.wait_ge(T.sem.ein1, 2)
+        act.wait_ge(T.sem.ein1, 2)
+        s1, s2 = T.ed1, T.ed2
+    if counting:
+        e_eb = one(syn, [], lambda: syn.dma_start(T.eb[0:16, 0:256], s1[:]), 16)
+    e_81 = one(act, [], lambda: act.dma_start(T.e8[:, 0:32], s1[:]), 16)
+    if not home:
+        act.wait_ge(T.sem.ein2, 2)
+    if second:
+        e_82 = one(act, [], lambda: act.dma_start(T.e8[:, 32:64], s2[:]), 16)
+
+    e_i1, e_i2, e_i3, e_i4 = ev(), ev(), ev(), ev()
+    do(e_i1, g.iota(T.iq[:], [[1, 1]], 0, 1))
+    do(e_i1, g.iota(C("fm"), [[0, 8], [1, 16]], 0, 0, **imp))
+    do(e_i2, g.iota(C("fd"), [[1, 8], [0, 16]], 0, 0, **imp))
+    e_c, e_x = [], []
+    if home:
+        pairs = _engines(topo.mask(core, helpers[0]))
+        pairs = [pairs[2 * i] | pairs[2 * i + 1] for i in range(len(helpers))]
+        for e, buf, sem in ((e_d1, T.ed1, "ein1"), (e_d2, T.ed2, "ein2")):
+            after(g, e)
+            fused([(buf[:], [(c, buf[:])], m, sem) for c, m in zip(helpers, pairs)])
+        e_go = issued()
+        for k in range(0, NS, 2):
+            q = (syn, act)[k // 2 % 2]
+            e_c.append(one(q, [e_go], lambda: q.dma_start(T.xd[k:k + 2], T.x[SR * k:SR * k + 2 * SR, :]), 16))
+    do(e_i2, g.iota(C("fi"), [[1, 128]], 0, 0, **imp))
+    do(e_i3, g.iota(C("f8"), [[0, 16], [1, 8]], 0, 0, **imp))
+    do(e_i3, g.iota(C("dump"), [[16, 32]], B8 + 1025, 1, **imp))
+    do(e_i3, g.iota(C("gx"), [[1, 136]], -8, 0, **imp))
+    do(e_i4, g.iota(C("um"), [[0, 9], [1, 16]], 0, 0, **imp))
+    if home:
+        for i in range(NS):
+            to = [helpers[i]] if i < len(helpers) else helpers
+            after(g, e_c[i // 2])
+            fused([(T.xd[i], [(c, T.xd[i]) for c in to], topo.mask(core, to[0]), "xs%d" % i)])
+        e_own = issued()
+        for k, q in enumerate((syn, act)):
+            a = slice(64 * k, 64 * k + 64)
+            e_x.append(one(q, [e_own], lambda: q.dma_start(T.xb[a, :], T.x[a, :]), 16))
+    do(e_i4, g.iota(C("da"), [[0, 32], [0, 2], [512, 8]], 0, 0, **imp))
+    do(e_i4, g.iota(C("db"), [[16, 32], [1, 2], [0, 8]], -256, 0, **imp))
+    if home:
+        e_i5 = ev()
+        do(e_i5, g.iota(C("pv"), [[16, 120]], 0, 0, **imp))
+        do(e_i5, g.iota(C("jj"), [[1, 8], [N - FULL, 2]], 0, 0, **imp))
+
+    e_rz = ev()
+    do(e_rz, vec.memset(T.rz[:], 1.0))
+    after(vec, e_i1)
+    k1 = ev()
+    for c, sc, op in ((0, 15, A.bitwise_and), (1, 4, A.arith_shift_right), (2, 7, A.bitwise_and)):
+        do(k1, ts(ti[:, c:c + 1], T.iq[:], sc, None, op))
+    do(k1, tc(tf[:, 0:1], T.iq[:]))
+    k2 = one(vec, [k1], lambda: tc(tf[:, 1:4], ti[:, 0:3]))
+    k3 = one(vec, [k2], lambda: ts(C("rr"), C("fm"), tf[:, 0:1], None, A.is_equal))
+    do(k3, ts(tf[:, 4:5], tf[:, 2:3], 8.0, None, A.add))
+    k4 = one(vec, [e_i2], lambda: ts(C("bo"), C("fd"), tf[:, 2:3], None, A.is_equal))
+    after(vec, e_i3, e_rz)
+    k5 = ev()
+    do(k5, vec.memset(T.rz[:, 0:1], 0.0))
+    do(k5, vec.memset(T.rz[:, 32:33], 0.0))
+    do(k5, ts(C("bo8"), C("f8"), tf[:, 3:4], None, A.is_equal))
+    do(k5, ts(C("pre8"), C("f8"), tf[:, 3:4], None, A.is_gt))
+    do(k5, ts(C("t3"), C("fi"), tf[:, 0:1], -1.0, A.is_lt, A.mult))
+    do(k5, ts(C("t5"), C("fi"), tf[:, 0:1], float(B8), A.is_equal, A.mult))
+    do(k5, ts(C("t6"), C("fi"), tf[:, 0:1], float(B8 + CAPP), A.is_equal, A.mult))
+    do(k5, ts(C("one"), C("fi"), 0.0, None, A.is_ge))
+    k6 = one(vec, [k5], lambda: tt(C("t4"), C("t3"), C("bo8"), A.mult))
+    after(vec, k6)
+    k7 = ev()
+    do(k7, tt(C("ua"), C("t4"), C("t5"), A.add))
+    do(k7, tt(C("ub"), C("t4"), C("t6"), A.add))
+    if second:
+        f0 = ev()
+        do(f0, ts(C("t1"), C("fi"), tf[:, 0:1], -1.0, A.is_le, A.mult))
+        do(f0, ts(C("t2"), C("fi"), tf[:, 0:1], float(BIG), A.is_equal, A.mult))
+        do(f0, ts(tf[:, 14:15], tf[:, 1:2], 8.0, None, A.mult))
+        do(f0, ts(C("neg", 0, 1), C("fi", 0, 1), 0.0, -1.0, A.is_ge, A.mult))
+        f1 = one(vec, [f0, k4], lambda: tt(C("t7"), C("t1"), C("bo"), A.mult))
+        do(f1, ts(C("ge"), C("gx"), tf[:, 14:15], None, A.is_equal))
+        f2 = one(vec, [f1], lambda: tt(C("up"), C("t7"), C("t2"), A.add))
+
+    if counting:
+        v0 = one(vec, [e_eb], lambda: tc(T.ef[0:16, :], T.eb[0:16, :]))
+        t0 = one(pe, [v0, k3], lambda: pe.matmul(T.pa[:, 0:256], C("rr", rows=16), T.ef[0:16, :], True, True))
+        after(vec, t0)
+        v1 = ev()
+        for h in range(2):
+            do(v1, ts(T.mm[:, 256 * h:256 * h + 256], T.pa[:, 0:256], tf[:, (2, 4)[h]:(3, 5)[h]], None, A.is_equal))
+        after(vec, v1)
+        v2 = ev()
+        for h in range(2):
+            a = slice(256 * h, 256 * h + 256)
+            do(v2, vec.tensor_tensor_scan(T.cu[:, a], T.mm[:, a], T.mm[:, a], 0.0, A.add, A.max))
+    if todo:
+        after(pe, v2, k4)
+        t1 = ev()
+        for h in range(2):
+            do(t1, pe.matmul(T.pc[0:1, 128 * h:128 * h + 128], T.cu[:, 256 * h + 255:256 * h + 256], C("bo"), True, True))
+        v3 = one(vec, [t1], lambda: tc(T.cs[0:1, :], T.pc[0:1, 0:256]))
+        e_cd = one(syn, [v3], lambda: syn.dma_start(T.cd[:], T.cs[0:1, :]), 16)
+        after(g, e_cd)
+        eng = _engines(topo.mask(core, todo[0]) & topo.mask(core, todo[-1]))
+        groups = [(eng[i], todo[i::len(eng)]) for i in range(min(len(eng), len(todo)))]
+        fused([(T.cd[:], [(c, T.cin[r]) for c in v], m, "cin") for m, v in groups])
+    if second:
+        after(pe, v2, f2, k4)
+        t2 = ev()
+        pe.matmul(T.pb[:], C("bo"), T.cu[:], True, False)
+        do(t2, pe.matmul(T.pb[:], C("up"), T.mm[:], False, True))
+        syn.wait_ge(T.sem.cin, r)
+        e_cl = one(syn, [], lambda: syn.dma_start(T.cl[0:r, :], T.cin[0:r]), 16)
+    if not home:
+        i = helpers.index(core)
+        n = _bits(topo.mask(R[r], core))
+        g.wait_ge(T.sem["xs%d" % i], n)
+        fused([(T.xd[i], [(c, T.xd[i]) for c in rest], topo.mask(core, rest[0]), "xs%d" % i)])
+        e_x.append(ev())
+        for h in [i] + [h for h in range(NS) if h != i]:
+            syn.wait_ge(T.sem["xs%d" % h], n)
+            do(e_x[0], syn.dma_start(T.xb[SR * h:SR * h + SR, :], T.xd[h]), 16)
+
+    k8 = ev()
+    do(k8, ts(tf[:, 8:9], tf[:, 1:2], 0.0, None, A.is_equal))
+    do(k8, ts(tf[:, 9:10], tf[:, 1:2], 1.0, None, A.is_equal))
+    do(k8, ts(tf[:, 10:11], tf[:, 1:2], 2.0, None, A.is_equal))
+    do(k8, ts(tf[:, 11:12], tf[:, 1:2], 2.0, None, A.is_lt))
+    do(k8, ts(tf[:, 12:13], tf[:, 2:3], 2.0, 256.0, A.mult, A.add))
+    e_w = [ev(), ev()]
+    do(e_w[0], vec.memset(T.qw1[:, 0:1040], 0.0))
+    if second:
+        do(e_w[1], vec.memset(T.qw2[:, 0:1040], 0.0))
+    after(vec, k8)
+    k9 = one(vec, [e_i4], lambda: ts(C("dc"), C("da"), tf[:, 8:9], tf[:, 10:11], A.mult, A.add))
+    do(k9, ts(C("de"), C("db"), tf[:, 9:10], None, A.mult))
+    do(k9, ts(tf[:, 13:14], tf[:, 10:11], tf[:, 12:13], tf[:, 11:12], A.mult, A.add))
+    after(vec, k9)
+    k10 = ev()
+    do(k10, tt(C("dd"), C("dc"), C("de"), A.add))
+    do(k10, ts(T.em[:], C("um"), 0.0, tf[:, 13:14], A.is_equal, A.mult))
+    e_win = ev()
+    if home:
+        do(e_win, vec.memset(T.win[:, ZERO:WIN], 0.0))
+        after(vec, e_i5)
+        h1 = ev()
+        do(h1, ts(C("pw"), C("pv"), tf[:, 1:2], None, A.add))
+        do(h1, ts(C("s8"), C("fm"), tf[:, 1:2], None, A.is_equal))
+        for k, add in ((0, 0.0), (1, 8.0), (2, -1.0), (3, 7.0)):
+            do(h1, ts(tf[:, 16 + k:17 + k], tf[:, 2:3], add, None, A.add))
+        do(h1, ts(tf[:, 20:21], tf[:, 2:3], 0.0, None, A.is_equal))
+        do(h1, ts(tf[:, 21:22], tf[:, 2:3], float(NB - 8), 20000.0, A.is_equal, A.mult))
+        do(h1, ts(tf[:, 22:23], tf[:, 2:3], float(NB - 8), float(BW), A.is_lt, A.mult))
+        after(vec, h1)
+        h2 = ev()
+        for k, op in ((0, A.is_lt), (1, A.is_lt), (2, A.is_equal), (3, A.is_equal)):
+            do(h2, ts(C("mk", 16 * k, 16 * k + 16), C("jj"), tf[:, 16 + k:17 + k], None, op))
+        do(h2, ts(C("pg0"), C("pw"), tf[:, 20:21], None, A.mult))
+        for x in range(2):
+            do(h2, ts(C("sc", x, x + 1), tf[:, 20:21], float(CAPP * x - BW), float(BW), A.mult, A.add))
+            do(h2, ts(C("sc", 2 + x, 3 + x), tf[:, 21:22], tf[:, 22:23], None, A.add))
+        bank = (T.pa, T.ph)
+        after(pe, h2)
+        if counting:
+            after(pe, v1)
+        h9 = ev()
+        for x in range(2):
+            do(h9, pe.matmul(bank[x][:, 0:120], C("s8"), C("pg0"), True, False))
+
+    held = {}
+
+    def number(k, m_ev):
+        k = str(k)
+        s = one(vec, [m_ev, k5], lambda: vec.tensor_tensor_scan(C("c" + k), T.rz[:], C("m" + k), 0.0, A.mult, A.add))
+        d1 = one(vec, [], lambda: tt(C("ms" + k), C("m" + k, 0, 32), C("m" + k, 32, 64), A.add))
+        after(pe, s, k5, *held.get("tot", []))
+        t = one(pe, [], lambda: pe.matmul(T.pe[:, 0:2], C("one"), C("c" + k, 31, 64, 32), True, True))
+        after(pe, k7, *held.get("z", []))
+        n = ev()
+        do(n, pe.matmul(T.pd[:, 64:66], C("pre8"), C("c" + k, 31, 64, 32), True, True))
+        for x in range(2):
+            a = (32 * x, 32 * x + 32)
+            pe.matmul(T.pd[:, a[0]:a[1]], C("bo8"), C("c" + k, *a), True, False)
+            do(n, pe.matmul(T.pd[:, a[0]:a[1]], C("ub" if x else "ua"), C("m" + k, *a), False, True))
+        d2 = one(vec, [d1], lambda: ts(C("dx" + k), C("ms" + k), -4096.0, None, A.mult))
+        d3 = one(vec, [d2], lambda: tt(C("dy" + k), C("dx" + k), C("dump"), A.add))
+        j = 2 * int(k)
+        tot = one(vec, [t], lambda: tc(T.cx[:, j - 2:j], T.pe[:, 0:2]))
+        after(vec, n)
+        z1 = ev()
+        for x in range(2):
+            a = (32 * x, 32 * x + 32)
+            do(z1, ts(C("z" + k, *a), T.pd[:, a[0]:a[1]], T.pd[:, 64 + x:65 + x], float(B8), A.add, A.max))
+        u = one(vec, [z1], lambda: tt(C("u" + k), C("z" + k, 0, 32), C("z" + k, 32, 64), A.max))
+        v = one(vec, [u, d3], lambda: tt(C("v" + k), C("u" + k), C("dy" + k), A.max))
+        o = one(vec, [v], lambda: ts(C("o" + k), C("v" + k), float(-B8), None, A.add))
+        held.update(tot=[tot], z=[z1])
+        return tot, o
+
+    def scatter(k, o):
+        return one(vec, [o, k10, e_w[k - 1]], lambda: tc(T["qw%d" % k][:, 0:WS].indirect(C("o%d" % k)), C("dd")))
+
+    def turn(k, sc):
+        after(pe, sc, k10, *held.get("l", []))
+        em = T.em
+        for b in range(16):
+            i = pe.matmul(T.pf[:, 0:64], em[:, 16 - b:144 - b], T["qw%d" % k][:, 1 + b:1010 + b:16], b == 0, b == 15)
+        e = ev()
+        do(e, i)
+        return e
+
+    def listed(k, x1):
+        l = one(vec, [x1], lambda: tc(C("l%d" % k), T.pf[:, 0:64]))
+        held["l"] = [l]
+        return l
+
+    def gathers(k, l, queues):
+        out = T.win if home else T["ob%d" % k]
+        a = BW * (r if k == 1 else N + r - FULL) if home else 0
+        e = ev()
+        for x, q in enumerate(queues):
+            after(q, l, *e_x)
+            win = T.xb[:, 0:4096].indirect(C("l%d" % k, 32 * x, 32 * x + 32))
+            to = out[:, a + CAPP * x:a + CAPP * x + CAPP]
+            do(e, act.activation(to, win, AF.Copy) if q is act else tc(to, win))
+        return e
+
+    after(vec, e_81)
+    m1 = ev()
+    for x in range(2):
+        do(m1, ts(C("m1", 32 * x, 32 * x + 32), T.e8[:, 0:32], float(2 * d + x), None, A.is_equal))
+    e_cz = ev()
+    if second:
+        after(vec, e_82)
+        e_m = ev()
+        for x in range(2):
+            do(e_m, ts(T.e2m[:, 32 * x:32 * x + 32], T.e8[:, 32:64], float(2 * d + x), None, A.is_equal))
+    else:
+        do(e_cz, vec.memset(T.cx[:, 2:4], 0.0))
+    tot1, o1 = number(1, m1)
+    tots = [tot1, e_cz]
+    if second:
+        after(pe, e_cl, f0)
+        t3 = ev()
+        for h in range(2):
+            do(t3, pe.matmul(T.pg[:, h:h + 1], T.cl[0:r, 128 * h:128 * h + 128], C("neg", 0, 1, rows=r), True, True))
+        f3 = one(vec, [t3], lambda: ts(T.thr[:], T.pg[:, 0:2], float(CAP + BIG), float(BIG), A.add, A.max))
+        after(vec, f3, t2)
+        f4 = ev()
+        for h in range(2):
+            a = slice(256 * h, 256 * h + 256)
+            do(f4, ts(T.ff[:, a], T.pb[:, a], T.thr[:, h:h + 1], None, A.is_ge))
+        sc1 = scatter(1, o1)
+        after(pe, f4, f1)
+        t4 = ev()
+        for i in range(16):
+            s, a = i % 8, 256 * (i // 8) + 32 * (i % 8)
+            ins = pe.matmul(T.pg[:, 32:64], C("ge", 8 - s, 136 - s), T.ff[:, a:a + 32], i == 0, i == 15)
+        do(t4, ins)
+        after(vec, t4, e_m)
+        m2 = ev()
+        for x in range(2):
+            a = (32 * x, 32 * x + 32)
+            do(m2, tt(C("m2", *a), T.pg[:, 32:64], T.e2m[:, a[0]:a[1]], A.mult))
+        tot2, o2 = number(2, m2)
+        tots = [tot1, tot2]
+        l1 = listed(1, turn(1, sc1))
+        sc2 = scatter(2, o2)
+        x2 = turn(2, sc2)
+    else:
+        l1 = listed(1, turn(1, scatter(1, o1)))
+    g1 = gathers(1, l1, (act, act))
+    if not home:
+        mask = topo.mask(core, R[d])
+        after(g, *[e for e in tots if e["n"]])
+        fused([(T.cx[:], [(R[d], T.cc[:, 4 * r:4 * r + 4])], mask, "ccs")])
+        after(g, g1)
+        fused([(T.ob1[:], [(R[d], T.win[:, BW * r:BW * r + BW])], mask, "wins")])
+        if second:
+            g2 = gathers(2, listed(2, x2), (vec, act))
+            after(g, g2)
+            a = BW * (N + r - FULL)
+            fused([(T.ob2[:], [(R[d], T.win[:, a:a + BW])], mask, "wins")])
+    else:
+        h0 = one(vec, [e for e in tots if e["n"]], lambda: tc(T.cc[:, 4 * r:4 * r + 4], T.cx[:]))
+        after(vec, h0, h2)
+        vec.wait_ge(T.sem.ccs, _arrivals(P, topo, r))
+        h3 = ev()
+        for x in range(2):
+            for k in range(4):
+                a = 64 * x + 16 * k
+                do(h3, tt(T.pr[:, a:a + 16], T.cc[:, x:32:2], C("mk", 16 * k, 16 * k + 16), A.mult))
+        after(vec, h3)
+        h4 = ev()
+        for k in range(4):
+            for x in range(2):
+                a = 64 * x + 16 * k
+                do(h4, vec.tensor_reduce(tf[:, 24 + 2 * k + x:25 + 2 * k + x], T.pr[:, a:a + 16], AxisListType.X, A.add))
+        h5 = one(vec, [h4], lambda: tt(C("sc", 4, 8), C("sc", 0, 4), tf[:, 28:32], A.subtract))
+        after(vec, h5)
+        h6 = [ev(), ev()]
+        for x in range(2):
+            for k in range(2):
+                a = 240 * x + 120 * k
+                do(h6[x], ts(T.aa[:, a:a + 120], C("pw"), tf[:, 24 + 2 * k + x:25 + 2 * k + x],
+                             C("sc", 4 + 2 * k + x, 5 + 2 * k + x), A.is_ge, A.mult))
+        h7, h8 = [ev(), ev()], [ev(), ev()]
+        for x in range(2):
+            after(pe, h6[x])
+            pe.matmul(bank[x][:, 0:120], C("s8"), T.aa[:, 240 * x:240 * x + 120], False, False)
+            do(h7[x], pe.matmul(bank[x][:, 0:120], C("s8"), T.aa[:, 240 * x + 120:240 * x + 240], False, True))
+        for x in range(2):
+            after(vec, h9, h7[x])
+            do(h8[x], ts(T.of[:, 120 * x:120 * x + 120], bank[x][:, 0:120], float(ZERO), None, A.min))
+        own = [g1, e_win]
+        if second:
+            own.append(gathers(2, listed(2, x2), (vec, act)))
+        for q, x in ((vec, 0), (act, 1)):
+            q.wait_ge(T.sem.wins, _arrivals(P, topo, r, [1] * FULL + [2] * (N - FULL)))
+            after(q, h8[x], *own)
+        stores = []
+        for a, b in ((0, 60), (60, 120)):
+            for x in range(2):
+                y, p = ev(), slice(CAP * x + 16 * a, CAP * x + 16 * b)
+                win = T.win[:, 0:WIN].indirect(T.of[:, 120 * x + a:120 * x + b])
+                do(y, act.activation(T.yo[:, p], win, AF.Copy) if x else tc(T.yo[:, p], win))
+                stores.append((y, p))
+        e_y = ev()
+        for y, p in stores:
+            after(syn, y)
+            do(e_y, syn.dma_start(T.y[:, p], T.yo[:, p]), 16)
+        after(syn, e_y)
     for e in evs:
         if not e["w"] and e["n"]:
             g.wait_ge(e["s"], e["n"])
     if sent[0]:
         g.wait_ge(T.sem.sent, sent[0])
-
-
-def _rank_core(g, core, T, topo, P, Q, r, ev, after, do, cols, send, fused):
-    vec, pe, act, syn = Q
-    R, brain = P["R"], P["brain"][r]
-    b0 = HEAD + r * BLK
-    e_e, e_pad = ev(), ev()
-    do(e_pad, vec.memset(T.win[:, 0:HEAD], 0.0))
-    do(e_pad, vec.memset(T.win[:, b0 + HALF:b0 + HALF + 1], 0.0))
-    do(e_pad, vec.memset(T.win[:, b0 + 4097:b0 + BLK], 0.0))
-    e_lw = ev()
-    do(e_lw, vec.memset(T.lw[:], 0.0))
-    do(e_e, syn.dma_start(T.eb[:, 0:32], T.e1[:]), 16)
-    do(e_e, act.dma_start(T.eb[:, 32:64], T.e2[:]), 16)
-    e_x = []
-    for k in range(4):
-        q = (syn, act)[k % 2]
-        e_x.append(ev())
-        after(q, e_pad)
-        a = b0 + 1024 * k + (1 if k >= 2 else 0)
-        do(e_x[k], q.dma_start(T.win[:, a:a + 1024], T.x[:, 1024 * k:1024 * k + 1024]), 16)
-    e_i = ev()
-    do(e_i, g.iota(T.ifq[:], [[1, 128]], 0, 0))
-    do(e_i, g.iota(T.iq[:], [[1, 1]], 0, 1))
-    do(e_i, g.iota(T.cib[:], [[0, 4], [16, 8]], -1, 0))
-    off = topo.mask(core, [c for c in R if topo.same_plane(core, c)][0])
-    after(g, e_e)
-    send(T.eb[:], T.eb[:], brain, topo.mask(core, brain) & off, "ein")
-    full = topo.mask(core, brain)
-    eng = [1 << i for i in range(16) if full >> i & 1]
-    quads = [sum(eng[i:i + 4]) for i in range(0, len(eng), 4)]
-    own = P["owner"][r]
-    for hs, need in ((range(0, 4), e_x[0:3]), (range(4, 8), e_x[2:4])):
-        hs = [h for h in hs if own[h] != core]
-        after(g, *need)
-        fused([(cols(r, h), [(own[h], cols(r, h))], quads[i], "x%d_%d" % (r, h)) for i, h in enumerate(hs)])
-    for s, h, d, mask, sem in P["sends"].get(core, []):
-        send(cols(s, h), cols(s, h), d, mask, sem)
-    tf, ti, kA = T.tf, T.ti, 2 * r
-    hh = kA // 8
-    after(vec, e_i)
-    c1 = ev()
-    do(c1, vec.tensor_scalar(ti[:, 0:1], T.iq[:], 15, None, A.bitwise_and))
-    do(c1, vec.tensor_scalar(ti[:, 1:2], T.iq[:], 4, None, A.arith_shift_right))
-    do(c1, vec.tensor_scalar(T.pmi[:], T.ifq[:], 15, None, A.bitwise_and))
-    do(c1, vec.tensor_copy(tf[:, 0:1], T.iq[:]))
-    after(vec, c1)
-    c2 = ev()
-    do(c2, vec.tensor_copy(tf[:, 1:2], ti[:, 0:1]))
-    do(c2, vec.tensor_copy(tf[:, 2:3], ti[:, 1:2]))
-    do(c2, vec.tensor_scalar(T.d2[:], T.ifq[:], tf[:, 0:1], None, A.subtract))
-    after(vec, c2)
-    c3 = ev()
-    do(c3, vec.tensor_scalar(T.dm[:], T.pmi[:], tf[:, 1:2], None, A.subtract))
-    do(c3, vec.tensor_scalar(tf[:, 3:4], tf[:, 2:3], float(r), None, A.is_equal))
-    do(c3, vec.tensor_scalar(tf[:, 8:16], T.ifq[:, 0:8], tf[:, 2:3], None, A.is_lt))
-    do(c3, vec.tensor_scalar(tf[:, 4:5], tf[:, 2:3], float(BLK), float(HEAD + HALF), A.mult, A.add))
-    for e in range(2):
-        do(c3, vec.tensor_scalar(tf[:, 5 + e:6 + e], tf[:, 0:1], float(16 * ((kA + e) % 8)), None, A.is_equal))
-    do(c3, vec.tensor_scalar(T.ci[:], T.cib[:], tf[:, 1:2], None, A.add))
-    after(vec, c3)
-    c4 = ev()
-    for e in range(2):
-        do(c4, vec.tensor_scalar(T.sel[:, 128 * e:128 * e + 128], T.ifq[:], 0.0, tf[:, 5 + e:6 + e], A.is_ge, A.mult))
-    for k in range(8):
-        do(c4, vec.tensor_scalar(T.mats[:, 128 * k:128 * k + 128], T.d2[:], float(16 * (k - r)), tf[:, 3:4], A.is_equal, A.mult))
-    after(pe, c4)
-    pe.wait_ge(T.sem.cnt2, 8 * _bits(off))
-    p1 = ev()
-    for e in range(2):
-        do(p1, pe.matmul(T.pa[:, 32 * e:32 * e + 32], T.sel[:, 128 * e:128 * e + 128], T.cc[:], True, True))
-    after(vec, p1)
-    s1 = ev()
-    for e in range(2):
-        nn, mm = T.pa[:, 32 * e + hh:32 * e + 32:4], T.pa[:, 32 * e + 2 + hh:32 * e + 32:4]
-        do(s1, vec.tensor_tensor(T.tm[:, 16 * e:16 * e + 8], nn, tf[:, 8:16], A.mult))
-        do(s1, vec.tensor_tensor(T.tm[:, 16 * e + 8:16 * e + 16], mm, tf[:, 8:16], A.mult))
-        do(s1, vec.tensor_reduce(tf[:, 16 + e:17 + e], nn, AxisListType.X, A.add))
-    after(vec, s1)
-    s2 = ev()
-    for e in range(2):
-        do(s2, vec.tensor_reduce(tf[:, 20 + e:21 + e], T.tm[:, 16 * e:16 * e + 8], AxisListType.X, A.add))
-        do(s2, vec.tensor_reduce(tf[:, 18 + e:19 + e], T.tm[:, 16 * e + 8:16 * e + 16], AxisListType.X, A.add))
-    do(s2, vec.tensor_scalar(tf[:, 24:26], tf[:, 16:18], 1920.0, None, A.min))
-    after(vec, s2)
-    s3 = ev()
-    do(s3, vec.tensor_tensor(tf[:, 22:24], tf[:, 24:26], tf[:, 18:20], A.add))
-    after(vec, s3)
-    s4 = ev()
-    do(s4, vec.tensor_copy(T.si[:, 0:4], tf[:, 20:24]))
-    after(vec, s4)
-    s5 = ev()
-    do(s5, vec.tensor_scalar(T.si[:, 4:8], T.si[:, 0:4], 4, None, A.arith_shift_right))
-    do(s5, vec.tensor_scalar(T.si[:, 8:12], T.si[:, 0:4], 15, None, A.bitwise_and))
-    after(vec, s5)
-    s6 = ev()
-    do(s6, vec.tensor_copy(tf[:, 26:30], T.si[:, 4:8]))
-    do(s6, vec.tensor_copy(tf[:, 30:34], T.si[:, 8:12]))
-    do(s6, vec.tensor_scalar(tf[:, 34:38], T.si[:, 8:12], -16.0, None, A.add))
-    after(vec, s6)
-    s7, s8 = ev(), ev()
-    for l in range(4):
-        do(s7, vec.tensor_scalar(T.cj[:, 8 * l:8 * l + 8], T.ci[:, 8 * l:8 * l + 8], tf[:, 26 + l:27 + l], -1.0, A.subtract, A.max))
-    for l in range(4):
-        for ab in range(2):
-            c, k = 30 + 4 * ab + l, 2 * (2 * l + ab)
-            do(s8, vec.tensor_scalar(T.rot[:, 128 * k:128 * k + 128], T.dm[:], tf[:, c:c + 1], None, A.is_equal))
-            do(s8, vec.tensor_scalar(T.rot[:, 128 * k + 128:128 * k + 256], T.dm[:], tf[:, c:c + 1], tf[:, 4:5], A.is_equal, A.mult))
-    after(vec, s7)
-    s9 = ev()
-    for l in range(4):
-        do(s9, vec.tensor_scalar(T.ix[:, 8 * l:8 * l + 8], T.cj[:, 8 * l:8 * l + 8], 32.0, float(34 * l + 1), A.min, A.add))
-    pe.wait_ge(T.sem.lists, 8 * _bits(off))
-    p2 = ev()
-    for k in range(8):
-        i = pe.matmul(T.pb[:, 0:128], T.mats[:, 128 * k:128 * k + 128], T.ls[:, 128 * k:128 * k + 128], k == 0, k == 7)
-    do(p2, i)
-    after(vec, p2, e_lw)
-    w1 = ev()
-    for l in range(4):
-        do(w1, vec.tensor_copy(T.lw[:, 34 * l + 1:34 * l + 33], T.pb[:, 32 * l:32 * l + 32]))
-    after(vec, w1, s9)
-    w2 = ev()
-    do(w2, vec.tensor_copy(T.gg[:], T.lw[:, 0:136].indirect(T.ix[:, 0:32])))
-    after(vec, w2)
-    w3 = ev()
-    do(w3, vec.tensor_scalar(T.gp[:], T.gg[:], 0.0, None, A.not_equal))
-    pw = [ev(), ev()]
-    bank = (T.pc, T.pd)
-    after(pe, s8, w2)
-    for k, src in ((0, T.gg), (1, T.gp)):
-        if k:
-            after(pe, w3)
-        for e in range(2):
-            for l in (e, 2 + e):
-                for ab in range(2):
-                    c = 128 * (2 * (2 * l + ab) + k)
-                    i = pe.matmul(bank[e][:, 0:120], T.rot[:, c:c + 128], src[:, 128 * l + 1 - ab:128 * l + 121 - ab],
-                                  k == 0 and l == e and ab == 0, k == 1 and l == 2 + e and ab == 1)
-            if k:
-                do(pw[e], i)
-    wo = [ev(), ev()]
-    for e in range(2):
-        after(vec, pw[e])
-        do(wo[e], vec.tensor_copy(T.ofs[:, 120 * e:120 * e + 120], bank[e][:, 0:120]))
-    for q, e in ((vec, 0), (act, 1)):
-        q.wait_ge(T.sem.xin, P["xin"][r])
-        after(q, e_pad, wo[e], *e_x)
-    stores = []
-    for k in range(2):
-        for e in range(2):
-            a, o = 1920 * e + 960 * k, 120 * e + 60 * k
-            y = ev()
-            win = T.win[:, 0:WIN].indirect(T.ofs[:, o:o + 60])
-            if e == 0:
-                do(y, vec.tensor_copy(T.yo[:, a:a + 960], win))
-            else:
-                do(y, act.activation(T.yo[:, a:a + 960], win, AF.Copy))
-            stores.append((y, a))
-    e_y = ev()
-    for y, a in stores:
-        after(syn, y)
-        do(e_y, syn.dma_start(T.y[:, a:a + 960], T.yo[:, a:a + 960]), 16)
-    after(syn, e_y)
-
-
-def _brain(g, core, T, topo, P, Q, r, ev, after, do, fused):
-    vec, pe, act, _ = Q
-    R, brains = P["R"], P["brain"]
-    tf, ti = T.tf, T.ti
-    off = topo.mask(core, [c for c in R if c != R[r]][0])
-    e_i = ev()
-    do(e_i, g.iota(T.ifq[:], [[1, 128]], 0, 0))
-    do(e_i, g.iota(T.iq[:], [[1, 1]], 0, 1))
-    do(e_i, g.iota(T.val[:], [[2049, 2], [1, 16]], -2048, 16, allow_small_or_imprecise_dtypes=True))
-    after(vec, e_i)
-    c1 = ev()
-    do(c1, vec.tensor_copy(tf[:, 0:1], T.iq[:]))
-    for c, sc, op in ((0, 15, A.bitwise_and), (1, 4, A.arith_shift_right), (2, 7, A.bitwise_and), (3, 3, A.arith_shift_right)):
-        do(c1, vec.tensor_scalar(ti[:, c:c + 1], T.iq[:], sc, None, op))
-    do(c1, vec.tensor_scalar(T.pmi[:], T.ifq[:], 15, None, A.bitwise_and))
-    do(c1, vec.tensor_scalar(T.gfi[:], T.ifq[:], 4, None, A.arith_shift_right))
-    do(c1, vec.tensor_copy(T.iot[:], T.ifq[:]))
-    after(vec, c1)
-    c2 = ev()
-    do(c2, vec.tensor_copy(tf[:, 1:5], ti[:, 0:4]))
-    do(c2, vec.tensor_scalar(T.d2[:], T.iot[:], tf[:, 0:1], None, A.subtract))
-    after(vec, c2)
-    c3 = ev()
-    for k, add in ((8, 8.0), (9, 64.0), (10, 72.0)):
-        do(c3, vec.tensor_scalar(tf[:, k:k + 1], tf[:, 2:3], add, None, A.add))
-    for k in range(8):
-        do(c3, vec.tensor_scalar(tf[:, 16 + k:17 + k], tf[:, 3:4], float(k), None, A.is_equal))
-    do(c3, vec.tensor_scalar(T.bo[:], T.gfi[:], tf[:, 2:3], None, A.is_equal))
-    do(c3, vec.tensor_scalar(T.gs[:], T.pmi[:], tf[:, 1:2], 64.0, A.is_equal, A.mult))
-    do(c3, vec.tensor_scalar(T.gt[:], T.ifq[:, 0:16], tf[:, 1:2], None, A.is_equal))
-    do(c3, vec.tensor_scalar(T.idb[:], T.d2[:], 0.0, None, A.is_equal))
-    do(c3, vec.tensor_scalar(T.idf[:], T.d2[:], 0.0, 2049.0, A.is_equal, A.mult))
-    do(c3, vec.tensor_scalar(T.u1[:], T.d2[:], 0.0, -1.0, A.is_le, A.mult))
-    after(vec, c3)
-    c4 = ev()
-    for k in range(8):
-        do(c4, vec.tensor_scalar(T.mats[:, 128 * k:128 * k + 128], T.pmi[:], tf[:, 4:5], tf[:, 16 + k:17 + k], A.is_equal, A.mult))
-    do(c4, vec.tensor_tensor(T.u1[:], T.u1[:], T.bo[:], A.mult))
-    after(vec, c4)
-    c7 = ev()
-    do(c7, vec.tensor_tensor(T.up[:], T.u1[:], T.idf[:], A.add))
-    vec.wait_ge(T.sem.ein, _bits(off))
-    v0 = ev()
-    do(v0, vec.tensor_copy(T.ef[:], T.eb[:]))
-    after(pe, c4, v0)
-    t0 = ev()
-    for w in range(2):
-        for k in range(8):
-            a = 256 * w + 32 * k
-            do(t0, pe.matmul(T.pa[:, a:a + 32], T.mats[:, 128 * k:128 * k + 128], T.ef[:, 32 * w:32 * w + 32], True, True))
-    after(vec, t0)
-    v1 = ev()
-    for h in range(2):
-        do(v1, vec.tensor_scalar(T.mm[:, 256 * h:256 * h + 256], T.pa[:, 0:256], tf[:, (2, 8)[h]:(3, 9)[h]], None, A.is_equal))
-    after(vec, v1)
-    v2 = ev()
-    for h in range(2):
-        a = slice(256 * h, 256 * h + 256)
-        do(v2, vec.tensor_tensor_scan(T.cu[:, a], T.mm[:, a], T.mm[:, a], 0.0, A.add, A.max))
-    after(pe, c7, v2)
-    t1, t2 = ev(), ev()
-    for h in range(2):
-        do(t1, pe.matmul(T.pe[:, h:h + 1], T.bo[:], T.cu[:, 256 * h + 255:256 * h + 256], True, True))
-    pe.matmul(T.pb[:], T.bo[:], T.cu[:], True, False)
-    do(t2, pe.matmul(T.pb[:], T.up[:], T.mm[:], False, True))
-    after(vec, t1)
-    v3 = ev()
-    do(v3, vec.tensor_copy(T.cs[:, 0:2], T.pe[:, 0:2]))
-    later = range(r + 1, len(R))
-    after(g, v3)
-    if later:
-        fused([(T.cs[:, 0:2], [(brains[k], T.cn[:, 2 * r:2 * r + 2]) for k in later], off, "cnt1")])
-    after(act, v1, t0)
-    a1 = ev()
-    do(a1, act.activation(T.er[:], T.pa[:], AF.Copy))
-    after(pe, a1)
-    t3, t4 = ev(), ev()
-    for w in range(2):
-        for cb in range(2):
-            do(t3, pe.matmul(T.pf[:, 32 * w + 16 * cb:32 * w + 16 * cb + 16], T.er[:, 256 * w + 128 * cb:256 * w + 128 * cb + 128],
-                             T.idb[:, 0:16], True, True))
-    pe.matmul(T.pc[:, 0:256], T.idb[:], T.er[:, 256:512], True, False)
-    after(vec, t2)
-    v4 = ev()
-    do(v4, vec.tensor_scalar(T.v1[:], T.pb[:], -2048.0, 0.0, A.add, A.max))
-
-    def per_token(bank, a, src, e):
-        for cb in range(2):
-            for h in range(2):
-                i = pe.matmul(bank[:, a + 16 * cb:a + 16 * cb + 16], src[:, 256 * h + 128 * cb:256 * h + 128 * cb + 128],
-                              T.gt[:], h == 0, h == 1)
-            do(e, i)
-    after(pe, v4)
-    per_token(T.pf, 64, T.v1, t4)
-    ki, kf = T.ki, T.kf
-
-    def c(k):
-        return slice(32 * k, 32 * k + 32)
-    after(vec, t3, t4)
-    k1 = ev()
-    do(k1, vec.tensor_copy(ki[:, 0:64], T.pf[:, 0:64]))
-    do(k1, vec.tensor_scalar(ki[:, c(2)], T.pf[:, 64:96], -1.0, None, A.add))
-    after(vec, k1)
-    k2 = ev()
-    do(k2, vec.tensor_scalar(ki[:, 96:160], ki[:, 0:64], 1, None, A.arith_shift_right))
-    do(k2, vec.tensor_scalar(ki[:, 160:224], ki[:, 0:64], 1, None, A.bitwise_and))
-    do(k2, vec.tensor_scalar(ki[:, c(7)], ki[:, c(2)], 15, None, A.bitwise_and))
-    do(k2, vec.tensor_scalar(ki[:, c(8)], ki[:, c(2)], 4, None, A.arith_shift_right))
-    after(vec, k2)
-    k3 = ev()
-    do(k3, vec.tensor_scalar(kf[:, 0:64], ki[:, 96:160], 16.0, None, A.mult))
-    do(k3, vec.tensor_scalar(kf[:, c(2)], ki[:, c(5)], 32.0, None, A.mult))
-    do(k3, vec.tensor_scalar(kf[:, c(3)], ki[:, c(6)], 32.0, 64.0, A.mult, A.add))
-    after(vec, k3)
-    k4 = ev()
-    do(k4, vec.tensor_tensor(kf[:, c(4)], kf[:, c(0)], ki[:, c(7)], A.add))
-    do(k4, vec.tensor_tensor(kf[:, c(5)], kf[:, c(2)], ki[:, c(8)], A.add))
-    after(vec, k4)
-    k5 = ev()
-    do(k5, vec.tensor_tensor(kf[:, c(6)], kf[:, c(1)], kf[:, c(4)], A.subtract))
-    do(k5, vec.tensor_tensor(kf[:, c(7)], kf[:, c(3)], kf[:, c(5)], A.subtract))
-    if r:
-        vec.wait_ge(T.sem.cnt1, r * _bits(off))
-        f1 = ev()
-        for h in range(2):
-            do(f1, vec.tensor_reduce(tf[:, 24 + h:25 + h], T.cn[:, h:2 * r:2], AxisListType.X, A.add, negate=True))
-        after(vec, f1)
-        f2 = ev()
-        do(f2, vec.tensor_scalar(tf[:, 26:28], tf[:, 24:26], 1920.0 + 2049.0, 2049.0, A.add, A.max))
-        after(vec, f2)
-    f3 = ev()
-    for h in range(2):
-        a = slice(256 * h, 256 * h + 256)
-        do(f3, vec.tensor_scalar(T.ff[:, a], T.pb[:, a], tf[:, 26 + h:27 + h] if r else 3969.0, None, A.is_ge))
-    after(pe, f3)
-    t5, t6 = ev(), ev()
-    pe.matmul(T.pc[:, 0:256], T.gs[:], T.ff[:, 0:256], False, False)
-    do(t5, pe.matmul(T.pc[:, 0:256], T.gs[:], T.ff[:, 256:512], False, True))
-    per_token(T.ph, 0, T.ff, t6)
-    after(vec, t5)
-    f4 = ev()
-    for h in range(2):
-        do(f4, vec.tensor_scalar(T.m2[:, 256 * h:256 * h + 256], T.pc[:, 0:256], tf[:, 9 + h:10 + h], None, A.is_equal))
-    after(vec, f4)
-    f5 = ev()
-    for h in range(2):
-        a = slice(256 * h, 256 * h + 256)
-        do(f5, vec.tensor_tensor_scan(T.c2[:, a], T.m2[:, a], T.m2[:, a], 0.0, A.add, A.max))
-    after(pe, f5)
-    t7, t8 = ev(), ev()
-    pe.matmul(T.pd[:], T.bo[:], T.c2[:], True, False)
-    do(t8, pe.matmul(T.pd[:], T.up[:], T.m2[:], False, True))
-    for h in range(2):
-        do(t7, pe.matmul(T.pe[:, 2 + h:3 + h], T.bo[:], T.c2[:, 256 * h + 255:256 * h + 256], True, True))
-    after(vec, t6, k5)
-    k6 = ev()
-    do(k6, vec.tensor_tensor(kf[:, c(8)], kf[:, c(6)], T.ph[:, 0:32], A.mult))
-    do(k6, vec.tensor_tensor(kf[:, c(9)], kf[:, c(7)], T.ph[:, 0:32], A.mult))
-    after(vec, k6)
-    k7 = ev()
-    do(k7, vec.tensor_tensor(kf[:, c(10)], kf[:, c(8)], kf[:, c(4)], A.add))
-    do(k7, vec.tensor_tensor(kf[:, c(11)], kf[:, c(9)], kf[:, c(5)], A.add))
-    after(vec, t8)
-    f6 = ev()
-    do(f6, vec.tensor_scalar(T.v2[:], T.pd[:], -2048.0, 0.0, A.add, A.max))
-    after(vec, t7)
-    f7 = ev()
-    do(f7, vec.tensor_copy(T.cs[:, 2:4], T.pe[:, 2:4]))
-    after(pe, f6, k6)
-    t9 = ev()
-    per_token(T.ph, 32, T.v2, t9)
-    after(g, f7)
-    fused([(T.cs[:, 0:4], [(d, T.cc[:, 4 * r:4 * r + 4]) for d in R], off, "cnt2")])
-    after(vec, t9)
-    k8 = ev()
-    do(k8, vec.tensor_scalar(ki[:, c(9)], T.ph[:, 32:64], -1.0, 0.0, A.add, A.max))
-    after(vec, k8)
-    k9 = ev()
-    do(k9, vec.tensor_scalar(ki[:, c(10)], ki[:, c(9)], 15, None, A.bitwise_and))
-    do(k9, vec.tensor_scalar(ki[:, c(11)], ki[:, c(9)], 4, None, A.arith_shift_right))
-    after(vec, k9, k7)
-    k10 = ev()
-    do(k10, vec.tensor_tensor(kf[:, c(12)], kf[:, c(10)], ki[:, c(10)], A.add))
-    do(k10, vec.tensor_tensor(kf[:, c(13)], kf[:, c(11)], ki[:, c(11)], A.add))
-    after(vec, k10)
-    for b0 in range(0, 32, 4):
-        o = ev()
-        for b in range(b0, b0 + 4):
-            a = slice(128 * b, 128 * b + 128)
-            do(o, vec.tensor_scalar(T.oh[:, a], T.iot[:], kf[:, 384 + b:385 + b], None, A.is_equal))
-            do(o, vec.tensor_scalar(T.ol[:, a], T.iot[:], kf[:, 416 + b:417 + b], T.val[:, b:b + 1], A.is_equal, A.mult))
-        after(pe, o)
-        for b in range(b0, b0 + 4):
-            a = slice(128 * b, 128 * b + 128)
-            i = pe.matmul(T.pg[:, 0:128], T.oh[:, a], T.ol[:, a], b == 0, b == 31)
-    t10 = ev()
-    do(t10, i)
-    after(vec, t10)
-    l1 = ev()
-    do(l1, vec.tensor_copy(T.lf[:], T.pg[:, 0:128]))
-    after(g, l1)
-    fused([(T.lf[:], [(d, T.ls[:, 128 * r:128 * r + 128]) for d in R], off, "lists")])

from concourse.bass import DstId, RemoteDMATransfer
from concourse.mybir import AluOpType as A, AxisListType, ActivationFunctionType as AF

N, CAP, CAPP = 8, 1920, 512
FULL = CAP // CAPP
BW = 2 * CAPP
NB = N + N - FULL
ZERO = NB * BW
WIN = ZERO + 16
NS, SR = 8, 16
BIG, B8 = 2049, 1024
WS = 1664
NEV = 110

F16, F32, I32, U16, BF = "float16", "float32", "int32", "uint16", "bfloat16"
SCRATCH = {
    "ed1": ("dram", [128, 32], I32), "ed2": ("dram", [128, 32], I32),
    "cd": ("dram", [128, 2], F16), "cin": ("dram", [8, 128, 2], F16), "xd": ("dram", [NS, 128, 512], BF),
    "xb": ("sbuf", [128, 4096], BF), "win": ("sbuf", [128, WIN], BF), "yo": ("sbuf", [128, 2 * CAP], BF),
    "ob1": ("sbuf", [128, BW], BF), "ob2": ("sbuf", [128, BW], BF),
    "eb": ("sbuf", [128, 256], I32), "e8": ("sbuf", [128, 64], I32), "ef": ("sbuf", [128, 256], F16),
    "iq": ("sbuf", [128, 1], I32), "ti": ("sbuf", [128, 4], I32), "tf": ("sbuf", [128, 64], F32),
    "em": ("sbuf", [128, 144], BF), "rz": ("sbuf", [128, 64], BF),
    "mm": ("sbuf", [128, 512], F16), "cu": ("sbuf", [128, 512], F16), "ff": ("sbuf", [128, 512], F16),
    "cs": ("sbuf", [128, 256], F16), "cl": ("sbuf", [128, 256], F16), "thr": ("sbuf", [128, 2], F32),
    "cx": ("sbuf", [128, 4], F32), "cc": ("sbuf", [128, 32], F32), "e2m": ("sbuf", [128, 64], F16),
    "pr": ("sbuf", [128, 128], F32), "aa": ("sbuf", [128, 480], F16), "of": ("sbuf", [128, 240], U16),
    "qw1": ("sbuf", [128, WS], BF), "qw2": ("sbuf", [128, WS], BF),
}
_AT = {}


def _share(buf, dtype, parts):
    at = 0
    for name, width in parts:
        _AT[name] = (buf, at, width)
        at += width
    SCRATCH[buf] = ("sbuf", [128, at], dtype)


_share("fx", F32, [("fi", 128), ("fm", 128), ("fd", 128), ("f8", 128), ("gx", 136), ("um", 144), ("dump", 32), ("pv", 120),
                   ("jj", 16), ("mk", 64), ("sc", 16), ("t2", 128)])
_share("dq", BF, [("da", 512), ("db", 512), ("dc", 512), ("de", 512), ("dd", 512)])
_share("kk", F16, [("rr", 128), ("bo", 128), ("up", 128), ("bo8", 128), ("pre8", 128), ("ua", 128), ("ub", 128), ("one", 128),
                   ("s8", 128), ("ge", 136), ("t1", 128), ("t3", 128), ("t4", 128), ("t5", 128), ("t6", 128), ("t7", 128),
                   ("pw", 120), ("pg0", 120), ("neg", 8)])
for _k in "12":
    _share("qf" + _k, F32, [("dx" + _k, 32), ("dy" + _k, 32), ("z" + _k, 64), ("u" + _k, 32), ("v" + _k, 32)])
    _share("qh" + _k, F16, [("m" + _k, 64), ("c" + _k, 64), ("ms" + _k, 32)])
    _share("qo" + _k, U16, [("o" + _k, 32), ("l" + _k, 64)])
for _n in "abcdefgh":
    SCRATCH["p" + _n] = ("psum", [128, 512], F32)
SEMAPHORES = ["e%d" % i for i in range(NEV)] + ["ein1", "ein2", "cin", "ccs", "wins", "sent"] + ["xs%d" % i for i in range(NS)]

_PLAN = {}


def _bits(m):
    return bin(m).count("1")


def _engines(m):
    return [1 << i for i in range(16) if m >> i & 1]


def _perms(v):
    return [[]] if not v else [[a] + p for i, a in enumerate(v) for p in _perms(v[:i] + v[i + 1:])]


def _plan(T, topo):
    if _PLAN:
        return _PLAN
    R, everyone = list(T.cores), range(256)

    def place(c):
        return (topo.host(c), topo.chip(c))
    chip = [[c for c in everyone if place(c) == place(R[r])] for r in range(N)]
    mate = [[c for c in everyone if topo.mates(c, R[r])][0] for r in range(N)]
    helpers = [[c for c in chip[r] if c != R[r]] for r in range(N)]
    cross, plain = [], []
    for r in range(N):
        cross.append([t for t in range(N) if t != r and not topo.same_plane(R[r], R[t])])
        plain.append([t for t in range(N) if topo.same_plane(R[r], R[t])])
    owners = [[c for c in helpers[r] if topo.may_write(c, mate[r])][:len(cross[r])] for r in range(N)]
    others = [[c for c in helpers[r] if c not in owners[r]][:len(plain[r])] for r in range(N)]

    def links(r, c, t):
        d = topo.die(c)
        if t in cross[r]:
            if topo.mates(R[r], R[t]):
                return [("mate", place(R[r]), d)]
            return [("mate", place(R[r]), d), ("out", place(mate[r]), d), ("in", place(R[t]), d)]
        return [("out", place(R[r]), d), ("in", place(R[t]), d)]
    pick = [(list(cross[r]), list(plain[r])) for r in range(N)]

    def uses(r, p):
        w = 2 if r >= FULL else 1
        return [(k, w) for c, t in list(zip(owners[r], p[0])) + list(zip(others[r], p[1])) for k in links(r, c, t)]
    for _ in range(3):
        for r in range(N):
            load = {}
            for s in range(N):
                if s != r:
                    for k, w in uses(s, pick[s]):
                        load[k] = load.get(k, 0) + w
            best = None
            for pa in _perms(cross[r]):
                for pb in _perms(plain[r]):
                    mine = {}
                    for k, w in uses(r, (pa, pb)):
                        mine[k] = mine.get(k, 0) + w
                    cost = sum((load.get(k, 0) + w) ** 2 - load.get(k, 0) ** 2 for k, w in mine.items())
                    if best is None or cost < best[0]:
                        best = (cost, (pa, pb))
            pick[r] = best[1]
    role = {}
    for r in range(N):
        role[R[r]] = (r, r)
        for c, t in list(zip(owners[r], pick[r][0])) + list(zip(others[r], pick[r][1])):
            role[c] = (r, t)
    cnt = {}
    for r in range(N):
        later = [s for s in range(r + 1, N) if s >= FULL]
        for s in sorted(later, key=lambda t: t in plain[r]):
            for d in chip[s]:
                able = [c for c in helpers[r] if topo.may_write(c, d)]
                c = min(able, key=lambda v: len(cnt.get(v, [])))
                cnt.setdefault(c, []).append(d)
    _PLAN.update(R=R, helpers=helpers, role=role, cnt=cnt)
    return _PLAN


def _arrivals(P, topo, t, times=None):
    return sum(_bits(topo.mask(c, P["R"][t])) * (times[r] if times else 1)
               for c, (r, d) in P["role"].items() if d == t and c != P["R"][t])


def rank_program(g, core, T, topo):
    P = _plan(T, topo)
    if core not in P["role"]:
        return
    R = P["R"]
    r, d = P["role"][core]
    home = core == R[r]
    helpers = P["helpers"][r]
    rest = [c for c in helpers if c != core]
    second = r >= FULL
    todo = P["cnt"].get(core, [])
    counting = todo or second
    vec, pe, act, syn = g.vector, g.tensor, g.scalar, g.sync
    QN = [(g, "g"), (vec, "v"), (pe, "t"), (act, "a"), (syn, "s")]
    evs, sent = [], [0]

    def C(name, a=0, b=None, step=1, rows=128):
        buf, at, width = _AT[name]
        return T[buf][0:rows, at + a:at + (width if b is None else b):step]

    def ev():
        e = {"s": T.sem["e%d" % len(evs)], "n": 0, "w": []}
        evs.append(e)
        return e

    def after(q, *deps):
        k = [b for a, b in QN if a is q][0]
        for e in deps:
            if k not in e["w"]:
                q.wait_ge(e["s"], e["n"])
                e["w"].append(k)

    def do(e, ins, n=1):
        ins.then_inc(e["s"], n)
        e["n"] += n

    def one(q, deps, make, n=1):
        after(q, *deps)
        e = ev()
        do(e, make(), n)
        return e

    def issued():
        e = ev()
        g.sem_inc(e["s"], 1)
        e["n"] += 1
        return e

    def dst(c):
        rid, pid = topo.addr(c, core)
        return DstId(rid=rid, pnc=pid)

    def fused(transfers):
        g.remote_dma_fused([RemoteDMATransfer(dst_ids=[dst(c) for c, _ in to], dma_engine_mask=mask, remote_sem=T.sem[sem],
                                              srcs=[a], dsts=[b for _, b in to]) for a, to, mask, sem in transfers],
                           local_sem=T.sem.sent)
        sent[0] += sum(_bits(mask) for _, _, mask, _ in transfers)

    tf, ti = T.tf, T.ti
    ts, tt, tc = vec.tensor_scalar, vec.tensor_tensor, vec.tensor_copy
    imp = {"allow_small_or_imprecise_dtypes": True}

    if home:
        e_d1 = one(syn, [], lambda: syn.dma_start(T.ed1[:], T.e1[:]), 16)
        e_d2 = one(act, [], lambda: act.dma_start(T.ed2[:], T.e2[:]), 16)
        s1, s2 = T.e1, T.e2
    else:
        syn.wait_ge(T.sem.ein1, 2)
        act.wait_ge(T.sem.ein1, 2)
        s1, s2 = T.ed1, T.ed2
    if counting:
        e_eb = one(syn, [], lambda: syn.dma_start(T.eb[0:16, 0:256], s1[:]), 16)
    e_81 = one(act, [], lambda: act.dma_start(T.e8[:, 0:32], s1[:]), 16)
    if not home:
        act.wait_ge(T.sem.ein2, 2)
    if second:
        e_82 = one(act, [], lambda: act.dma_start(T.e8[:, 32:64], s2[:]), 16)

    e_i1, e_i2, e_i3, e_i4 = ev(), ev(), ev(), ev()
    do(e_i1, g.iota(T.iq[:], [[1, 1]], 0, 1))
    do(e_i1, g.iota(C("fm"), [[0, 8], [1, 16]], 0, 0, **imp))
    do(e_i2, g.iota(C("fd"), [[1, 8], [0, 16]], 0, 0, **imp))
    e_c, e_x = [], []
    if home:
        pairs = _engines(topo.mask(core, helpers[0]))
        pairs = [pairs[2 * i] | pairs[2 * i + 1] for i in range(len(helpers))]
        for e, buf, sem in ((e_d1, T.ed1, "ein1"), (e_d2, T.ed2, "ein2")):
            after(g, e)
            fused([(buf[:], [(c, buf[:])], m, sem) for c, m in zip(helpers, pairs)])
        e_go = issued()
        for k in range(0, NS, 2):
            q = (syn, act)[k // 2 % 2]
            e_c.append(one(q, [e_go], lambda: q.dma_start(T.xd[k:k + 2], T.x[SR * k:SR * k + 2 * SR, :]), 16))
    do(e_i2, g.iota(C("fi"), [[1, 128]], 0, 0, **imp))
    do(e_i3, g.iota(C("f8"), [[0, 16], [1, 8]], 0, 0, **imp))
    do(e_i3, g.iota(C("dump"), [[16, 32]], B8 + 1025, 1, **imp))
    do(e_i3, g.iota(C("gx"), [[1, 136]], -8, 0, **imp))
    do(e_i4, g.iota(C("um"), [[0, 9], [1, 16]], 0, 0, **imp))
    if home:
        for i in range(NS):
            to = [helpers[i]] if i < len(helpers) else helpers
            after(g, e_c[i // 2])
            fused([(T.xd[i], [(c, T.xd[i]) for c in to], topo.mask(core, to[0]), "xs%d" % i)])
        e_own = issued()
        for k, q in enumerate((syn, act)):
            a = slice(64 * k, 64 * k + 64)
            e_x.append(one(q, [e_own], lambda: q.dma_start(T.xb[a, :], T.x[a, :]), 16))
    do(e_i4, g.iota(C("da"), [[0, 32], [0, 2], [512, 8]], 0, 0, **imp))
    do(e_i4, g.iota(C("db"), [[16, 32], [1, 2], [0, 8]], -256, 0, **imp))
    if home:
        e_i5 = ev()
        do(e_i5, g.iota(C("pv"), [[16, 120]], 0, 0, **imp))
        do(e_i5, g.iota(C("jj"), [[1, 8], [N - FULL, 2]], 0, 0, **imp))

    e_rz = ev()
    do(e_rz, vec.memset(T.rz[:], 1.0))
    after(vec, e_i1)
    k1 = ev()
    for c, sc, op in ((0, 15, A.bitwise_and), (1, 4, A.arith_shift_right), (2, 7, A.bitwise_and)):
        do(k1, ts(ti[:, c:c + 1], T.iq[:], sc, None, op))
    do(k1, tc(tf[:, 0:1], T.iq[:]))
    k2 = one(vec, [k1], lambda: tc(tf[:, 1:4], ti[:, 0:3]))
    k3 = one(vec, [k2], lambda: ts(C("rr"), C("fm"), tf[:, 0:1], None, A.is_equal))
    do(k3, ts(tf[:, 4:5], tf[:, 2:3], 8.0, None, A.add))
    k4 = one(vec, [e_i2], lambda: ts(C("bo"), C("fd"), tf[:, 2:3], None, A.is_equal))
    after(vec, e_i3, e_rz)
    k5 = ev()
    do(k5, vec.memset(T.rz[:, 0:1], 0.0))
    do(k5, vec.memset(T.rz[:, 32:33], 0.0))
    do(k5, ts(C("bo8"), C("f8"), tf[:, 3:4], None, A.is_equal))
    do(k5, ts(C("pre8"), C("f8"), tf[:, 3:4], None, A.is_gt))
    do(k5, ts(C("t3"), C("fi"), tf[:, 0:1], -1.0, A.is_lt, A.mult))
    do(k5, ts(C("t5"), C("fi"), tf[:, 0:1], float(B8), A.is_equal, A.mult))
    do(k5, ts(C("t6"), C("fi"), tf[:, 0:1], float(B8 + CAPP), A.is_equal, A.mult))
    do(k5, ts(C("one"), C("fi"), 0.0, None, A.is_ge))
    k6 = one(vec, [k5], lambda: tt(C("t4"), C("t3"), C("bo8"), A.mult))
    after(vec, k6)
    k7 = ev()
    do(k7, tt(C("ua"), C("t4"), C("t5"), A.add))
    do(k7, tt(C("ub"), C("t4"), C("t6"), A.add))
    if second:
        f0 = ev()
        do(f0, ts(C("t1"), C("fi"), tf[:, 0:1], -1.0, A.is_le, A.mult))
        do(f0, ts(C("t2"), C("fi"), tf[:, 0:1], float(BIG), A.is_equal, A.mult))
        do(f0, ts(tf[:, 14:15], tf[:, 1:2], 8.0, None, A.mult))
        do(f0, ts(C("neg", 0, 1), C("fi", 0, 1), 0.0, -1.0, A.is_ge, A.mult))
        f1 = one(vec, [f0, k4], lambda: tt(C("t7"), C("t1"), C("bo"), A.mult))
        do(f1, ts(C("ge"), C("gx"), tf[:, 14:15], None, A.is_equal))
        f2 = one(vec, [f1], lambda: tt(C("up"), C("t7"), C("t2"), A.add))

    if counting:
        v0 = one(vec, [e_eb], lambda: tc(T.ef[0:16, :], T.eb[0:16, :]))
        t0 = one(pe, [v0, k3], lambda: pe.matmul(T.pa[:, 0:256], C("rr", rows=16), T.ef[0:16, :], True, True))
        after(vec, t0)
        v1 = ev()
        for h in range(2):
            do(v1, ts(T.mm[:, 256 * h:256 * h + 256], T.pa[:, 0:256], tf[:, (2, 4)[h]:(3, 5)[h]], None, A.is_equal))
        after(vec, v1)
        v2 = ev()
        for h in range(2):
            a = slice(256 * h, 256 * h + 256)
            do(v2, vec.tensor_tensor_scan(T.cu[:, a], T.mm[:, a], T.mm[:, a], 0.0, A.add, A.max))
    if todo:
        after(pe, v2, k4)
        t1 = ev()
        for h in range(2):
            do(t1, pe.matmul(T.pc[0:1, 128 * h:128 * h + 128], T.cu[:, 256 * h + 255:256 * h + 256], C("bo"), True, True))
        v3 = one(vec, [t1], lambda: tc(T.cs[0:1, :], T.pc[0:1, 0:256]))
        e_cd = one(syn, [v3], lambda: syn.dma_start(T.cd[:], T.cs[0:1, :]), 16)
        after(g, e_cd)
        eng = _engines(topo.mask(core, todo[0]) & topo.mask(core, todo[-1]))
        groups = [(eng[i], todo[i::len(eng)]) for i in range(min(len(eng), len(todo)))]
        fused([(T.cd[:], [(c, T.cin[r]) for c in v], m, "cin") for m, v in groups])
    if second:
        after(pe, v2, f2, k4)
        t2 = ev()
        pe.matmul(T.pb[:], C("bo"), T.cu[:], True, False)
        do(t2, pe.matmul(T.pb[:], C("up"), T.mm[:], False, True))
        syn.wait_ge(T.sem.cin, r)
        e_cl = one(syn, [], lambda: syn.dma_start(T.cl[0:r, :], T.cin[0:r]), 16)
    if not home:
        i = helpers.index(core)
        n = _bits(topo.mask(R[r], core))
        g.wait_ge(T.sem["xs%d" % i], n)
        fused([(T.xd[i], [(c, T.xd[i]) for c in rest], topo.mask(core, rest[0]), "xs%d" % i)])
        e_x.append(ev())
        for h in [i] + [h for h in range(NS) if h != i]:
            syn.wait_ge(T.sem["xs%d" % h], n)
            do(e_x[0], syn.dma_start(T.xb[SR * h:SR * h + SR, :], T.xd[h]), 16)

    k8 = ev()
    do(k8, ts(tf[:, 8:9], tf[:, 1:2], 0.0, None, A.is_equal))
    do(k8, ts(tf[:, 9:10], tf[:, 1:2], 1.0, None, A.is_equal))
    do(k8, ts(tf[:, 10:11], tf[:, 1:2], 2.0, None, A.is_equal))
    do(k8, ts(tf[:, 11:12], tf[:, 1:2], 2.0, None, A.is_lt))
    do(k8, ts(tf[:, 12:13], tf[:, 2:3], 2.0, 256.0, A.mult, A.add))
    e_w = [ev(), ev()]
    do(e_w[0], vec.memset(T.qw1[:, 0:1040], 0.0))
    if second:
        do(e_w[1], vec.memset(T.qw2[:, 0:1040], 0.0))
    after(vec, k8)
    k9 = one(vec, [e_i4], lambda: ts(C("dc"), C("da"), tf[:, 8:9], tf[:, 10:11], A.mult, A.add))
    do(k9, ts(C("de"), C("db"), tf[:, 9:10], None, A.mult))
    do(k9, ts(tf[:, 13:14], tf[:, 10:11], tf[:, 12:13], tf[:, 11:12], A.mult, A.add))
    after(vec, k9)
    k10 = ev()
    do(k10, tt(C("dd"), C("dc"), C("de"), A.add))
    do(k10, ts(T.em[:], C("um"), 0.0, tf[:, 13:14], A.is_equal, A.mult))
    e_win = ev()
    if home:
        do(e_win, vec.memset(T.win[:, ZERO:WIN], 0.0))
        after(vec, e_i5)
        h1 = ev()
        do(h1, ts(C("pw"), C("pv"), tf[:, 1:2], None, A.add))
        do(h1, ts(C("s8"), C("fm"), tf[:, 1:2], None, A.is_equal))
        for k, add in ((0, 0.0), (1, 8.0), (2, -1.0), (3, 7.0)):
            do(h1, ts(tf[:, 16 + k:17 + k], tf[:, 2:3], add, None, A.add))
        do(h1, ts(tf[:, 20:21], tf[:, 2:3], 0.0, None, A.is_equal))
        do(h1, ts(tf[:, 21:22], tf[:, 2:3], float(NB - 8), 20000.0, A.is_equal, A.mult))
        do(h1, ts(tf[:, 22:23], tf[:, 2:3], float(NB - 8), float(BW), A.is_lt, A.mult))
        after(vec, h1)
        h2 = ev()
        for k, op in ((0, A.is_lt), (1, A.is_lt), (2, A.is_equal), (3, A.is_equal)):
            do(h2, ts(C("mk", 16 * k, 16 * k + 16), C("jj"), tf[:, 16 + k:17 + k], None, op))
        do(h2, ts(C("pg0"), C("pw"), tf[:, 20:21], None, A.mult))
        for x in range(2):
            do(h2, ts(C("sc", x, x + 1), tf[:, 20:21], float(CAPP * x - BW), float(BW), A.mult, A.add))
            do(h2, ts(C("sc", 2 + x, 3 + x), tf[:, 21:22], tf[:, 22:23], None, A.add))
        bank = (T.pa, T.ph)
        after(pe, h2)
        if counting:
            after(pe, v1)
        h9 = ev()
        for x in range(2):
            do(h9, pe.matmul(bank[x][:, 0:120], C("s8"), C("pg0"), True, False))

    held = {}

    def number(k, m_ev):
        k = str(k)
        s = one(vec, [m_ev, k5], lambda: vec.tensor_tensor_scan(C("c" + k), T.rz[:], C("m" + k), 0.0, A.mult, A.add))
        d1 = one(vec, [], lambda: tt(C("ms" + k), C("m" + k, 0, 32), C("m" + k, 32, 64), A.add))
        after(pe, s, k5, *held.get("tot", []))
        t = one(pe, [], lambda: pe.matmul(T.pe[:, 0:2], C("one"), C("c" + k, 31, 64, 32), True, True))
        after(pe, k7, *held.get("z", []))
        n = ev()
        do(n, pe.matmul(T.pd[:, 64:66], C("pre8"), C("c" + k, 31, 64, 32), True, True))
        for x in range(2):
            a = (32 * x, 32 * x + 32)
            pe.matmul(T.pd[:, a[0]:a[1]], C("bo8"), C("c" + k, *a), True, False)
            do(n, pe.matmul(T.pd[:, a[0]:a[1]], C("ub" if x else "ua"), C("m" + k, *a), False, True))
        d2 = one(vec, [d1], lambda: ts(C("dx" + k), C("ms" + k), -4096.0, None, A.mult))
        d3 = one(vec, [d2], lambda: tt(C("dy" + k), C("dx" + k), C("dump"), A.add))
        j = 2 * int(k)
        tot = one(vec, [t], lambda: tc(T.cx[:, j - 2:j], T.pe[:, 0:2]))
        after(vec, n)
        z1 = ev()
        for x in range(2):
            a = (32 * x, 32 * x + 32)
            do(z1, ts(C("z" + k, *a), T.pd[:, a[0]:a[1]], T.pd[:, 64 + x:65 + x], float(B8), A.add, A.max))
        u = one(vec, [z1], lambda: tt(C("u" + k), C("z" + k, 0, 32), C("z" + k, 32, 64), A.max))
        v = one(vec, [u, d3], lambda: tt(C("v" + k), C("u" + k), C("dy" + k), A.max))
        o = one(vec, [v], lambda: ts(C("o" + k), C("v" + k), float(-B8), None, A.add))
        held.update(tot=[tot], z=[z1])
        return tot, o

    def scatter(k, o):
        return one(vec, [o, k10, e_w[k - 1]], lambda: tc(T["qw%d" % k][:, 0:WS].indirect(C("o%d" % k)), C("dd")))

    def turn(k, sc):
        after(pe, sc, k10, *held.get("l", []))
        em = T.em
        for b in range(16):
            i = pe.matmul(T.pf[:, 0:64], em[:, 16 - b:144 - b], T["qw%d" % k][:, 1 + b:1010 + b:16], b == 0, b == 15)
        e = ev()
        do(e, i)
        return e

    def listed(k, x1):
        l = one(vec, [x1], lambda: tc(C("l%d" % k), T.pf[:, 0:64]))
        held["l"] = [l]
        return l

    def gathers(k, l, queues):
        out = T.win if home else T["ob%d" % k]
        a = BW * (r if k == 1 else N + r - FULL) if home else 0
        e = ev()
        for x, q in enumerate(queues):
            after(q, l, *e_x)
            win = T.xb[:, 0:4096].indirect(C("l%d" % k, 32 * x, 32 * x + 32))
            to = out[:, a + CAPP * x:a + CAPP * x + CAPP]
            do(e, act.activation(to, win, AF.Copy) if q is act else tc(to, win))
        return e

    after(vec, e_81)
    m1 = ev()
    for x in range(2):
        do(m1, ts(C("m1", 32 * x, 32 * x + 32), T.e8[:, 0:32], float(2 * d + x), None, A.is_equal))
    e_cz = ev()
    if second:
        after(vec, e_82)
        e_m = ev()
        for x in range(2):
            do(e_m, ts(T.e2m[:, 32 * x:32 * x + 32], T.e8[:, 32:64], float(2 * d + x), None, A.is_equal))
    else:
        do(e_cz, vec.memset(T.cx[:, 2:4], 0.0))
    tot1, o1 = number(1, m1)
    tots = [tot1, e_cz]
    if second:
        after(pe, e_cl, f0)
        t3 = ev()
        for h in range(2):
            do(t3, pe.matmul(T.pg[:, h:h + 1], T.cl[0:r, 128 * h:128 * h + 128], C("neg", 0, 1, rows=r), True, True))
        f3 = one(vec, [t3], lambda: ts(T.thr[:], T.pg[:, 0:2], float(CAP + BIG), float(BIG), A.add, A.max))
        after(vec, f3, t2)
        f4 = ev()
        for h in range(2):
            a = slice(256 * h, 256 * h + 256)
            do(f4, ts(T.ff[:, a], T.pb[:, a], T.thr[:, h:h + 1], None, A.is_ge))
        sc1 = scatter(1, o1)
        after(pe, f4, f1)
        t4 = ev()
        for i in range(16):
            s, a = i % 8, 256 * (i // 8) + 32 * (i % 8)
            ins = pe.matmul(T.pg[:, 32:64], C("ge", 8 - s, 136 - s), T.ff[:, a:a + 32], i == 0, i == 15)
        do(t4, ins)
        after(vec, t4, e_m)
        m2 = ev()
        for x in range(2):
            a = (32 * x, 32 * x + 32)
            do(m2, tt(C("m2", *a), T.pg[:, 32:64], T.e2m[:, a[0]:a[1]], A.mult))
        tot2, o2 = number(2, m2)
        tots = [tot1, tot2]
        l1 = listed(1, turn(1, sc1))
        sc2 = scatter(2, o2)
        x2 = turn(2, sc2)
    else:
        l1 = listed(1, turn(1, scatter(1, o1)))
    g1 = gathers(1, l1, (act, act))
    if not home:
        mask = topo.mask(core, R[d])
        after(g, *[e for e in tots if e["n"]])
        fused([(T.cx[:], [(R[d], T.cc[:, 4 * r:4 * r + 4])], mask, "ccs")])
        after(g, g1)
        fused([(T.ob1[:], [(R[d], T.win[:, BW * r:BW * r + BW])], mask, "wins")])
        if second:
            g2 = gathers(2, listed(2, x2), (vec, act))
            after(g, g2)
            a = BW * (N + r - FULL)
            fused([(T.ob2[:], [(R[d], T.win[:, a:a + BW])], mask, "wins")])
    else:
        h0 = one(vec, [e for e in tots if e["n"]], lambda: tc(T.cc[:, 4 * r:4 * r + 4], T.cx[:]))
        after(vec, h0, h2)
        vec.wait_ge(T.sem.ccs, _arrivals(P, topo, r))
        h3 = ev()
        for x in range(2):
            for k in range(4):
                a = 64 * x + 16 * k
                do(h3, tt(T.pr[:, a:a + 16], T.cc[:, x:32:2], C("mk", 16 * k, 16 * k + 16), A.mult))
        after(vec, h3)
        h4 = ev()
        for k in range(4):
            for x in range(2):
                a = 64 * x + 16 * k
                do(h4, vec.tensor_reduce(tf[:, 24 + 2 * k + x:25 + 2 * k + x], T.pr[:, a:a + 16], AxisListType.X, A.add))
        h5 = one(vec, [h4], lambda: tt(C("sc", 4, 8), C("sc", 0, 4), tf[:, 28:32], A.subtract))
        after(vec, h5)
        h6 = [ev(), ev()]
        for x in range(2):
            for k in range(2):
                a = 240 * x + 120 * k
                do(h6[x], ts(T.aa[:, a:a + 120], C("pw"), tf[:, 24 + 2 * k + x:25 + 2 * k + x],
                             C("sc", 4 + 2 * k + x, 5 + 2 * k + x), A.is_ge, A.mult))
        h7, h8 = [ev(), ev()], [ev(), ev()]
        for x in range(2):
            after(pe, h6[x])
            pe.matmul(bank[x][:, 0:120], C("s8"), T.aa[:, 240 * x:240 * x + 120], False, False)
            do(h7[x], pe.matmul(bank[x][:, 0:120], C("s8"), T.aa[:, 240 * x + 120:240 * x + 240], False, True))
        for x in range(2):
            after(vec, h9, h7[x])
            do(h8[x], ts(T.of[:, 120 * x:120 * x + 120], bank[x][:, 0:120], float(ZERO), None, A.min))
        own = [g1, e_win]
        if second:
            own.append(gathers(2, listed(2, x2), (vec, act)))
        for q, x in ((vec, 0), (act, 1)):
            q.wait_ge(T.sem.wins, _arrivals(P, topo, r, [1] * FULL + [2] * (N - FULL)))
            after(q, h8[x], *own)
        stores = []
        for a, b in ((0, 60), (60, 120)):
            for x in range(2):
                y, p = ev(), slice(CAP * x + 16 * a, CAP * x + 16 * b)
                win = T.win[:, 0:WIN].indirect(T.of[:, 120 * x + a:120 * x + b])
                do(y, act.activation(T.yo[:, p], win, AF.Copy) if x else tc(T.yo[:, p], win))
                stores.append((y, p))
        e_y = ev()
        for y, p in stores:
            after(syn, y)
            do(e_y, syn.dma_start(T.y[:, p], T.yo[:, p]), 16)
        after(syn, e_y)
    for e in evs:
        if not e["w"] and e["n"]:
            g.wait_ge(e["s"], e["n"])
    if sent[0]:
        g.wait_ge(T.sem.sent, sent[0])
